import numpy as np, ml_dtypes
CORES = [1,5,17,21,33,37,49,53]
N = 8
BF = ml_dtypes.bfloat16
def f(rng, *shape):
    return (rng.standard_normal(shape, dtype=np.float32) * np.exp2(rng.integers(-2, 3, shape[:-1] + (1,)))).astype(BF)
def wide(rng, *shape):
    v = f(rng, *shape).astype(np.float32); k = shape[:-2] + (1, shape[-1])
    return (v * np.exp2(rng.integers(-6, 7, k)) * (rng.random(k) > 0.0625)).astype(BF)
def gentries(a):
    return np.ascontiguousarray(a.reshape(8, 16, -1).transpose(0, 2, 1)).reshape(8, -1)
def gtable(e):
    e = np.asarray(e); return np.ascontiguousarray(e.reshape(8, -1, 16).transpose(0, 2, 1)).reshape(128, -1).astype(np.int32)
M, I, Q, W = 4096, 256, 1024, 4096
CAPT, CAP = 31, 192
def parts(rng, n, lo, hi):
    room = rng.permutation(np.repeat(np.arange(len(lo)), hi - lo))[:n - int(np.sum(lo))]
    return lo + np.bincount(room, minlength=len(lo))
def ticks(rng, kind=""):
    times = np.zeros((N, 8, M), np.int32); own = np.zeros((N, 8, M), np.int64)
    for s in range(N):
        for g in range(8):
            lo = rng.integers(0, (M - 2 * CAPT) // I + 1, I); hi = np.full(I, CAPT, np.int64); o = rng.permutation(I)
            if kind == "full":
                lo[:] = 0; lo[o[:M // CAPT]] = CAPT
            else:
                c, z = o[:2], o[2:2 + I // 16]
                if kind == "ends":
                    c, z = (np.array([0, I - 1]), o[:0]) if s % 2 == 0 else (o[:0], np.array([0, I - 1]))
                lo[c] = CAPT; lo[z] = 0; hi[z] = 0
            own[s, g] = rng.permutation(np.repeat(np.arange(I), parts(rng, M, lo, hi)))
            t = rng.integers(0, W, M); t = np.where(rng.random(M) < 0.5, t, t - t % (W // 64))
            if kind == "ties":
                t = np.concatenate([[0, W - 1], rng.integers(0, W, 14)])[rng.integers(0, 16, M)]
            if kind == "ends":
                if rng.random() < 0.5:
                    t[0] = 0; t[1] = W - 1
                else:
                    t = W // 4 + t // 2
            times[s, g] = s * W + np.sort(t)
    return times, own
def index(own):
    pm = np.stack([gtable(np.argsort(own[s], axis=1, kind="stable")) for s in range(N)])
    starts = np.zeros((N, 8, I + 1), np.int32)
    for s in range(N):
        for g in range(8):
            starts[s, g, 1:] = np.add.accumulate(np.bincount(own[s, g], minlength=I))
    return pm, starts
def queries(rng, times, own, full=False):
    qi = np.zeros((N, 8, Q), np.int32); qt = np.zeros((N, 8, Q), np.int32)
    for r in range(N):
        a, b = rng.choice(8, 2, replace=False)
        for g in range(8):
            lo = np.zeros(N, np.int64); hi = np.full(N, CAP, np.int64); o = (r + 1 + rng.permutation(N - 1)) % N
            if full:
                if g % 2 == 1:
                    o = np.concatenate([[r], o])
                lo[o[:Q // CAP]] = CAP
            elif g == a:
                lo[o[0]] = CAP
            elif g == b:
                hi[o[0]] = 0
            s = rng.permutation(np.repeat(np.arange(N), parts(rng, Q, lo, hi)))
            k = rng.integers(0, M, Q); u = rng.random(Q)
            i = np.where(u < 0.5, own[s, g, k], rng.integers(0, I, Q))
            t = np.where((u > 0.25) & (u < 0.75), times[s, g, k], s * W + rng.integers(0, W, Q))
            t = np.where((u > 0.4) & (u < 0.5), np.maximum(t - 1, s * W), t)
            qi[r, g] = i; qt[r, g] = t
    return qi, qt
def sparse(rng, v):
    keep = rng.random((N, 128, M), dtype=np.float32) < np.exp2(-rng.integers(1, 7, (N, 128, 1)))
    return np.where(keep, v.astype(np.float32), np.float32(0)).astype(BF)
def make(rng, kind=""):
    times, own = ticks(rng, kind); pm, starts = index(own); qi, qt = queries(rng, times, own, kind == "full")
    return {"x": sparse(rng, f(rng, N, 128, M)), "times": times, "pm": pm, "starts": starts, "qi": qi, "qt": qt}
def setup_inputs(rng):
    return make(rng)
def setup_inputs_ends(rng):
    d = make(rng, "ends"); qt = d["qt"].astype(np.int64); s = qt // W; g = np.arange(8)[None, :, None]
    first = d["times"][s, g, 0].astype(np.int64); last = d["times"][s, g, M - 1].astype(np.int64)
    c = rng.integers(0, 6, qt.shape)
    t = np.choose(c, [s * W, s * W + W - 1, np.maximum(first - 1, s * W), np.minimum(last + 1, s * W + W - 1), last, qt])
    e = rng.random(qt.shape)
    d["qi"] = np.where(e < 0.25, 0, np.where(e < 0.5, I - 1, d["qi"])).astype(np.int32); d["qt"] = t.astype(np.int32); return d
def setup_inputs_full(rng):
    return make(rng, "full")
def setup_inputs_ties(rng):
    return make(rng, "ties")
def setup_inputs_old(rng):
    d = make(rng); h = np.where(rng.random(128) < 0.5, 0, rng.integers(0, N, 128))
    keep = (np.arange(N)[:, None] == h)[:, :, None] & (rng.random((N, 128, M), dtype=np.float32) < 0.25)
    d["x"] = np.where(keep, f(rng, N, 128, M).astype(np.float32), np.float32(0)).astype(BF); return d
def setup_inputs_spread(rng):
    d = make(rng); d["x"] = sparse(rng, wide(rng, N, 128, M)); return d
def check_inputs(d):
    bad = []; t = d["times"].astype(np.int64); st = d["starts"].astype(np.int64); qi = d["qi"]; qt = d["qt"].astype(np.int64)
    e = np.stack([gentries(a) for a in d["pm"]]).astype(np.int64); s0 = (np.arange(N) * W)[:, None, None]
    size = np.abs(d["x"].astype(np.float32))
    if not np.isfinite(size).all(): bad.append("x finite")
    if not ((size == 0) | (size >= 2.0 ** -100)).all(): bad.append("x size")
    if not ((t >= s0) & (t < s0 + W)).all(): bad.append("times in the slice")
    if not (np.diff(t, axis=2) >= 0).all(): bad.append("times in order")
    n = np.diff(st, axis=2)
    if not ((st[:, :, 0] == 0).all() and (st[:, :, I] == M).all() and (n >= 0).all()): bad.append("starts")
    else:
        if not (n <= CAPT).all(): bad.append("ticks of an instrument")
        for s in range(N):
            for g in range(8):
                edge = np.zeros(M + 1, bool); edge[st[s, g]] = True
                if not ((np.diff(e[s, g]) > 0) | edge[1:M]).all() and "pm in order" not in bad: bad.append("pm in order")
    if not (np.sort(e, axis=2) == np.arange(M)).all(): bad.append("pm a permutation")
    if not ((qi >= 0) & (qi < I)).all(): bad.append("qi range")
    if not ((qt >= 0) & (qt < N * W)).all(): bad.append("qt range")
    if not all((np.sum(qt // W == s, axis=2) <= CAP).all() for s in range(N)): bad.append("queries in a slice")
    return bad
def reference(x, times, pm, starts, qi, qt):
    y = np.zeros((N, 8, 16, Q), np.float32)
    for g in range(8):
        i = qi[:, g].reshape(-1).astype(np.int64); key = i * (N * W) + qt[:, g].reshape(-1)
        v = np.zeros((16, N * Q), np.float32)
        for s in range(N):
            e = gentries(pm[s])[g]; st = starts[s, g].astype(np.int64)
            w = x[s, 16 * g:16 * g + 16].astype(np.float32)[:, e]
            p = np.searchsorted(np.repeat(np.arange(I), np.diff(st)) * (N * W) + times[s, g][e], key, "right")
            last = np.maximum.accumulate(np.where(w != 0, np.arange(M), -1), axis=1)
            last = np.concatenate([np.full((16, 1), -1, np.int64), last], axis=1)[:, p]
            v = np.where(last >= st[i], np.take_along_axis(w, np.maximum(last, 0), axis=1), v)
        y[:, g] = v.reshape(16, N, Q).transpose(1, 0, 2)
    return {"y": y.reshape(N, 128, Q).astype(BF)}

@@ -1,0 +1,491 @@
+from concourse.bass import DstId, RemoteDMATransfer
+from concourse.mybir import AluOpType as A, ActivationFunctionType as AF
+
+N, M, I, Q, CAP = 8, 4096, 256, 1024, 192
+S = N * CAP
+BIG = 65536.0
+F0 = 16
+BF, F32, I32, U16 = "bfloat16", "float32", "int32", "uint16"
+
+SCRATCH = {}
+for _n, _w, _d in [
+    ("zero", 512, BF), ("b128", 128, BF), ("l2", 128, BF), ("zz", 144, BF), ("zf", 144, F32), ("uu", 2048, BF),
+    ("r0", 512, BF), ("m0", 512, BF), ("pen16", 352, BF), ("t16", 128, BF), ("pent", 352, BF), ("dump", 16, I32),
+    ("stb", 16, I32), ("tb", 256, I32), ("pm32", 256, I32), ("pm16", 256, U16),
+    ("qtin", 64, I32), ("sb", 32, BF), ("tc", 512, BF),
+    ("src", Q, I32), ("qwin", S, F32), ("stwin", 272, BF), ("twin", M, BF), ("tg", M, BF),
+    ("s1", 64, BF), ("sw", 64, BF), ("ee", 512, BF), ("cin", 512, BF), ("mx", 512, F32), ("a192", 64, F32),
+    ("slf", 64, F32), ("slot", 64, U16), ("slot2", 64, U16), ("qs", 96, I32), ("qr", 96, I32),
+    ("se", 32, I32), ("w1", 64, I32), ("w2", 64, I32), ("w3", 64, I32), ("w4", 32, I32),
+    ("kl", 48, U16), ("pl", 48, U16), ("offs", 16, U16), ("offr", 16, U16),
+    ("xw", M, BF), ("xs", M, BF), ("mk", M + 368, BF), ("ff", M + F0, BF),
+    ("pen", 768, BF), ("kk", 272, F32), ("tt", 768, F32),
+    ("ii", 96, I32), ("il", 96, U16), ("tq", 96, I32), ("th", 96, BF), ("tl", 96, BF),
+    ("trep", S, F32), ("ca", S, BF), ("cc", S, BF), ("sg", S, BF),
+    ("o1", 96, F32), ("o2", 96, F32), ("o3", 96, F32), ("off", 96, U16),
+    ("ans", S, BF), ("al", S, BF), ("sl", 7 * I, BF), ("i0", 8 * I, BF), ("i1", 8 * I, BF), ("pp", 8 * I, BF),
+    ("q8", 96, I32), ("pidx", 96, U16),
+    ("d0", 2 * S, BF), ("d1", 2 * S, BF), ("oo", 2 * S, BF), ("yo", Q, BF),
+]:
+    SCRATCH[_n] = ("sbuf", [128, _w], _d)
+for _k in range(8):
+    SCRATCH["p%d" % _k] = ("psum", [128, 512], F32)
+
+SEMAPHORES = ["qarr", "sarr", "sarr2", "aarr0", "aarr1", "sent"] + ["e%d" % _k for _k in range(100)]
+
+
+def peers(T, topo, r):
+    c = T.cores
+    rot = [(r + k) % N for k in range(1, N)]
+    far = [o for o in rot if topo.chip(c[o]) != topo.chip(c[r])]
+    near = [o for o in rot if topo.chip(c[o]) == topo.chip(c[r])]
+    return far, near
+
+
+def bits(engines):
+    return sum(1 << e for e in engines)
+
+
+def two_calls(T, topo, r, near_call):
+    c = T.cores
+    far, near = peers(T, topo, r)
+    off = topo.engines(c[r], c[far[0]])
+    on = [e for e in topo.engines(c[r], c[near[0]]) if e not in off]
+    q, h = len(off) // 4, len(off) // 2
+    calls = [[(far[k], off[k * q:(k + 1) * q]) for k in range(4)],
+             [(far[4 + k], off[k * h:(k + 1) * h]) for k in range(2)]]
+    calls[near_call].append((near[0], on))
+    return calls
+
+
+def place(T, topo, o, r):
+    far, near = peers(T, topo, o)
+    return (far + near + [o]).index(r)
+
+
+def runs(blocks):
+    out = []
+    for b in sorted(blocks):
+        if out and out[-1][1] == b:
+            out[-1] = (out[-1][0], b + 1)
+        else:
+            out.append((b, b + 1))
+    return out
+
+
+def rank_program(g, core, T, topo):
+    rank = T.rank_of(core)
+    if rank is None:
+        return
+    V, SC, PE, SY = g.vector, g.scalar, g.tensor, g.sync
+    evs = []
+
+    def ev():
+        e = [T.sem["e%d" % len(evs)], 0, 0]
+        evs.append(e)
+        return e
+
+    def inc(ins, e, n=1):
+        ins.then_inc(e[0], n)
+        e[1] += n
+        return e
+
+    def one(ins, n=1):
+        return inc(ins, ev(), n)
+
+    def wait(q, *es):
+        for e in es:
+            if e[1] > 0:
+                q.wait_ge(e[0], e[1])
+                e[2] = e[1]
+
+    cv, cg = ev(), ev()
+
+    def v(ins):
+        inc(ins, cv)
+
+    def vs():
+        wait(V, cv)
+
+    def dst(o):
+        a = topo.addr(T.cores[o])
+        return DstId(rid=a[0], pnc=a[1])
+
+    sent = [T.sem.sent, 0, 0]
+
+    def fused(items, sem):
+        g.remote_dma_fused([RemoteDMATransfer(dst_ids=[dst(o) for o in os_], dma_engine_mask=bits(en), remote_sem=sem,
+                                              srcs=[s], dsts=[d] * len(os_)) for os_, en, s, d in items],
+                           local_sem=sent[0])
+        sent[1] += sum(len(en) for _, en, _, _ in items)
+
+    def wrap(out, rhs_of, e, first=True, last=True, z=T.zz):
+        for r in range(16):
+            inc(PE.matmul(out, z[:, 15 - r:143 - r], rhs_of(r), first and r == 0, last and r == 15), e)
+        return e
+
+    far, near = peers(T, topo, rank)
+
+    e_st, e_qtin, e_tb, e_pm, e_x, e_src = ev(), ev(), ev(), ev(), ev(), ev()
+    for blk in range(2):
+        for g2 in range(2):
+            k = blk * 32 + g2 * 16
+            inc(SY.dma_start(T.qtin[:, k:k + 16], T.qt[g2::2, 512 * blk:512 * blk + 512]), e_qtin, 16)
+    inc(SY.dma_start(T.pm32[:], T.pm[:]), e_pm, 16)
+    inc(SY.dma_start(T.stb[:], T.starts[:, 0:I]), e_st, 16)
+    e_zero = one(V.memset(T.zero[:], 0.0))
+    e_s0 = one(V.memset(T.src[:], 0))
+    wait(SY, e_s0)
+    inc(SY.dma_start(T.src[0::16, :], T.qi[:]), e_src, 16)
+    inc(SY.dma_start(T.src[1::16, :], T.qt[:]), e_src, 16)
+    inc(SY.dma_start(T.xw[:], T.x[:]), e_x, 16)
+    inc(SY.dma_start(T.tb[:], T.times[:]), e_tb, 16)
+
+    e_z0, e_i1 = ev(), ev()
+    inc(V.memset(T.zz[:], 0.0), e_z0)
+    inc(V.memset(T.zf[:], 0.0), e_z0)
+    e_w0 = one(V.memset(T.stwin[:, 0:I], 0.0))
+    e_st256 = one(V.memset(T.stwin[:, I:272], float(M // 16)))
+    v(V.memset(T.r0[:], 1.0))
+    v(V.memset(T.m0[:], 1.0))
+    v(V.memset(T.kk[:, 256:272], 0.0))
+    v(V.memset(T.ff[:, 0:F0], 0.0))
+    v(V.memset(T.i0[:, 0::8], 0.0))
+    v(V.memset(T.i1[:, 0::8], 0.0))
+    vs()
+    v(V.memset(T.r0[:, 0::64], 0.0))
+    v(V.memset(T.m0[:, 0::8], 0.0))
+
+    wait(g, e_zero)
+    blk16 = [[-16, 8], [0, 16]]
+    inc(g.affine_select(T.b128[:], T.zero[:, 0:128], blk16, A.is_ge, 1.0, -16, 1), cg)
+    inc(g.affine_select(T.l2[:], T.zero[:, 0:128], [[1, 128]], A.is_ge, -1.0, 0, -1), cg)
+    wait(g, cg)
+    e_b128 = one(g.affine_select(T.b128[:], T.b128[:], blk16, A.is_ge, 0.0, 0, 1))
+    inc(g.affine_select(T.l2[:], T.l2[:], [[16, 8], [0, 16]], A.is_ge, 0.0, 15, -1), cg)
+    wait(g, cg)
+    e_l2 = one(g.affine_select(T.l2[:], T.l2[:], [[-1, 128]], A.not_equal, 2048.0, 0, 1))
+    inc(g.affine_select(T.pen16[0:16, 0:272], T.zero[0:16, 0:272], [[-1, 16], [0, 17]], A.is_ge, BIG, 0, 1), cg)
+    e_p16 = ev()
+    inc(g.affine_select(T.pen16[0:16, 272:352], T.zero[0:16, 0:80], [[1, 80]], A.is_ge, BIG, -33, -1), e_p16)
+    inc(g.affine_select(T.t16[0:16, :], T.zero[0:16, 0:128], [[0, 8], [-1, 16]], A.not_equal, 1.0, 0, 1), e_p16)
+    wait(g, cg)
+    inc(g.affine_select(T.pen16[0:16, 0:272], T.pen16[0:16, 0:272], [[0, 16], [1, 17]], A.is_ge, BIG, -1, -1), e_p16)
+    e_dump = one(g.iota(T.dump[:], [[16, 16]], M - 8192, 1))
+
+    wait(SC, e_zero)
+    e_qw0, e_tw0, e_d0 = ev(), ev(), ev()
+    for k in range(S // 512):
+        inc(SC.activation(T.qwin[:, 512 * k:512 * k + 512], T.zero[:], AF.Copy), e_qw0)
+    wait(SC, e_z0, e_b128)
+    e_z = one(SC.activation(T.zz[:, 15:143:16], T.b128[:, 0::16], AF.Copy))
+    e_zf0 = one(SC.activation(T.zf[:, 15:143:16], T.b128[:, 0::16], AF.Copy))
+    for k in range(M // 512):
+        inc(SC.activation(T.twin[:, 512 * k:512 * k + 512], T.zero[:], AF.Copy), e_tw0)
+    for k in range(S // 512):
+        inc(SC.activation(T.d0[:, 1024 * k:1024 * k + 1024:2], T.zero[:], AF.Copy), e_d0)
+    wait(g, e_zf0)
+    e_zf = one(g.affine_select(T.zf[:, 15:143:16], T.zf[:, 15:143:16], [[-16, 8]], A.not_equal, 32768.0, 0, 1))
+    e_u = ev()
+
+    def make_u(k):
+        inc(g.affine_select(T.uu[:, 512 * k:512 * k + 512], T.zero[:], [[-1, 4], [-16, 8], [0, 16]],
+                            A.not_equal, 1.0, -4 * k, 1), e_u)
+    for k in range(4):
+        make_u(k)
+
+    wait(V, e_qtin)
+    v(V.tensor_scalar(T.s1[:], T.qtin[:], 1.0 / 4096, 191.5 + 1.0 / 8192, A.mult, A.add))
+    vs()
+    v(V.transpose(T.sw[:], T.s1[:]))
+    vs()
+    e_e = ev()
+    for s in range(N):
+        inc(V.tensor_scalar(T.ee[:, 64 * s:64 * s + 64], T.sw[:], float(192 + s), None, A.is_equal), e_e)
+    wait(V, e_e)
+    e_cin = one(V.tensor_tensor_scan(T.cin[:], T.r0[:], T.ee[:], 0.0, A.mult, A.add))
+    wait(PE, e_b128, e_l2, e_e, e_cin)
+    e_d = ev()
+    for s in range(N):
+        inc(PE.matmul(T.p0[:, s::8], T.l2[:], T.ee[:, 64 * s:64 * s + 64], True, False), e_d)
+        inc(PE.matmul(T.p0[:, s::8], T.b128[:], T.cin[:, 64 * s:64 * s + 64], False, True), e_d)
+    v(V.tensor_scalar(T.a192[:], T.sw[:], float(CAP), -float(192 * CAP + 2049), A.mult, A.add))
+    wait(V, e_st)
+    e_c1 = one(V.tensor_copy(T.sb[:, 0:16], T.stb[:]))
+    wait(V, e_pm)
+    e_pm16 = one(V.tensor_copy(T.pm16[:], T.pm32[:]))
+    wait(V, e_c1)
+    e_c2 = one(V.tensor_tensor(T.sb[:, 16:32], T.stb[:], T.sb[:, 0:16], A.subtract))
+    wait(SY, e_w0, e_c1, e_c2)
+    e_stw = ev()
+    for k in range(2):
+        inc(SY.dma_start(T.stwin[k::16, 0:I], T.sb[:, 16 * k:16 * k + 16]), e_stw, 16)
+    wait(V, e_d)
+    v(V.tensor_tensor_scan(T.mx[:], T.m0[:], T.p0[:], 0.0, A.mult, A.max))
+    vs()
+    v(V.tensor_tensor(T.slf[:], T.mx[:, 7::8], T.a192[:], A.add))
+    vs()
+    e_slot = one(V.tensor_copy(T.slot[:], T.slf[:]))
+    wait(V, e_slot, e_src, e_qw0)
+    e_scat = one(V.tensor_copy(T.qwin[:, 0:S].indirect(T.slot[:, 0:64]), T.src[:]))
+
+    wait(V, e_tb)
+    e_t1 = one(V.tensor_copy(T.tc[:, 0:256], T.tb[:]))
+    e_slot2 = one(V.tensor_scalar(T.slot2[:], T.slf[:], 2.0, 1.0, A.mult, A.add))
+    wait(V, e_t1)
+    e_t2 = one(V.tensor_tensor(T.tc[:, 256:512], T.tb[:], T.tc[:, 0:256], A.subtract))
+    wait(SY, e_tw0, e_t1, e_t2)
+    e_tw = ev()
+    for k in range(2):
+        inc(SY.dma_start(T.twin[k::16, :], T.tc[:, 256 * k:256 * k + 256]), e_tw, 16)
+
+    wait(PE, e_p16)
+    e_pp = one(PE.matmul(T.p7[:, 0:352], T.t16[0:16, :], T.pen16[0:16, :], True, True))
+    wait(PE, e_z, e_stw, e_st256)
+    e_se = ev()
+    wrap(T.p6[:, 0:16], lambda r: T.stwin[:, r:I:16], e_se)
+    wrap(T.p6[:, 16:32], lambda r: T.stwin[:, r + 1:I + 1:16], e_se)
+    wait(PE, e_scat, e_zf)
+    e_qwrap = wrap(T.p1[:, 0:96], lambda r: T.qwin[:, r::16], ev(), z=T.zf)
+
+    wait(SC, e_pp)
+    e_pent = one(SC.activation(T.pent[:], T.p7[:, 0:352], AF.Copy))
+    wait(SC, e_pm16, e_x)
+    e_xs = []
+    for k in range(4):
+        e_xs.append(one(SC.activation(T.xs[:, 1024 * k:1024 * k + 1024],
+                                      T.xw[:, 0:M].indirect(T.pm16[:, 64 * k:64 * k + 64]), AF.Copy)))
+
+    wait(V, e_se)
+    v(V.tensor_copy(T.se[:], T.p6[:, 0:32]))
+    vs()
+    st, en = T.se[:, 0:16], T.se[:, 16:32]
+    v(V.tensor_scalar(T.w1[:, 0:16], st, 4, None, A.arith_shift_right))
+    v(V.tensor_scalar(T.w1[:, 16:32], st, 15, None, A.bitwise_and))
+    v(V.tensor_scalar(T.w1[:, 32:48], st, 0x1FF0, None, A.bitwise_and))
+    v(V.tensor_tensor(T.w1[:, 48:64], en, st, A.subtract))
+    vs()
+    e_kl, e_pl = ev(), ev()
+    for k, h in enumerate((1, 0, 2)):
+        inc(V.tensor_scalar(T.kl[:, 16 * k:16 * k + 16], T.w1[:, 0:16], float(h), None, A.add), e_kl)
+    v(V.tensor_tensor(T.w2[:, 0:16], en, T.w1[:, 32:48], A.subtract))
+    v(V.tensor_scalar(T.w2[:, 16:32], T.w1[:, 16:32], 17.0, None, A.mult))
+    v(V.tensor_scalar(T.w2[:, 32:48], T.w1[:, 48:64], 1.0, 8192.0, A.min, A.mult))
+    vs()
+    inc(V.tensor_scalar(T.pl[:, 0:16], T.w2[:, 0:16], 288.0, None, A.add), e_pl)
+    inc(V.tensor_scalar(T.pl[:, 32:48], T.w2[:, 0:16], 272.0, None, A.add), e_pl)
+    v(V.tensor_scalar(T.w3[:, 0:16], T.w2[:, 0:16], 16.0, None, A.min))
+    v(V.tensor_tensor(T.w3[:, 16:32], T.w2[:, 32:48], en, A.add))
+    v(V.tensor_tensor(T.w3[:, 32:48], st, T.w2[:, 32:48], A.subtract))
+    wait(V, e_dump)
+    vs()
+    v(V.tensor_tensor(T.w4[:, 0:16], T.w3[:, 0:16], T.w2[:, 16:32], A.add))
+    v(V.tensor_tensor(T.w4[:, 16:32], T.w3[:, 32:48], T.dump[:], A.min))
+    v(V.tensor_scalar(T.offs[:], T.w3[:, 16:32], float(F0 - 1 - 8192), 0.0, A.add, A.max))
+    vs()
+    inc(V.tensor_copy(T.pl[:, 16:32], T.w4[:, 0:16]), e_pl)
+    v(V.tensor_scalar(T.offr[:], T.w4[:, 16:32], 8192.0, None, A.add))
+
+    def mask(k):
+        wait(V, e_xs[k])
+        v(V.tensor_scalar(T.mk[:, 1024 * k:1024 * k + 1024], T.xs[:, 1024 * k:1024 * k + 1024], 0.0, None, A.is_equal))
+    mask(0)
+
+    wait(V, e_qwrap)
+    e_qs = one(V.tensor_copy(T.qs[:], T.p1[:, 0:96]))
+    e_qown = one(V.tensor_copy(T.qr[:, 84:96], T.p1[:, 12 * rank:12 * rank + 12]))
+    wait(g, e_qs)
+    for call in two_calls(T, topo, rank, 0):
+        fused([([o], en_, T.qs[:, 12 * o:12 * o + 12],
+                T.qr[:, 12 * place(T, topo, o, rank):12 * place(T, topo, o, rank) + 12]) for o, en_ in call], T.sem.qarr)
+
+    for k in range(1, 4):
+        mask(k)
+    vs()
+    v(V.tensor_copy(T.mk[:, 0:M + 368].indirect(T.offr[:, 0:16]), T.zero[:, 0:I]))
+    vs()
+    e_ff = one(V.tensor_tensor_scan(T.ff[:, F0:F0 + M], T.mk[:, 0:M], T.xs[:], 0.0, A.mult, A.add))
+    ffw = T.ff[:, 0:F0 + M]
+    e_sown = ev()
+    die = [topo.die(c) for c in T.cores]
+    order = sorted(range(N - 1), key=lambda r: (die[r], r))
+    off = topo.engines(core, T.cores[far[0]])
+    if rank < N - 1:
+        mine = T.sl[:, I * order.index(rank):I * order.index(rank) + I]
+        wait(V, e_ff)
+        inc(V.tensor_copy(mine, ffw.indirect(T.offs[:, 0:16])), e_sown)
+        wait(g, e_sown)
+        fused([([o for o in far if die[o] == die[rank]], off, mine, mine)], T.sem.sarr)
+    same = [order.index(r) for r in order if die[r] == die[rank]]
+    sarr = [T.sem.sarr, len(off) * len([r for r in order if die[r] == die[rank] and r != rank]), 0]
+    wait(g, sarr)
+    block = T.sl[:, I * same[0]:I * same[-1] + I]
+    fused([(near, topo.engines(core, T.cores[near[0]]), block, block)], T.sem.sarr2)
+    sarr2 = [T.sem.sarr2, len(topo.engines(T.cores[near[0]], core)), 0]
+
+    wait(SC, e_tw)
+    e_tg = []
+    for k in range(3):
+        e_tg.append(one(SC.activation(T.tg[:, 1024 * k:1024 * k + 1024],
+                                      T.twin[:, 0:M].indirect(T.pm16[:, 64 * k:64 * k + 64]), AF.Copy)))
+        if k == 0:
+            wait(SC, e_pl, e_pent)
+            e_pen = one(SC.activation(T.pen[:], T.pent[:, 0:352].indirect(T.pl[:, 0:48]), AF.Copy))
+    wait(V, e_tw, e_pm16)
+    e_tg.append(one(V.tensor_copy(T.tg[:, 3072:M], T.twin[:, 0:M].indirect(T.pm16[:, 192:256]))))
+    e_kw, e_uw = ev(), [ev(), ev(), ev()]
+    for k in range(4):
+        wait(PE, e_tg[k])
+        wrap(T.p5[:, 64 * k:64 * k + 64], lambda r: T.tg[:, 1024 * k + r:1024 * k + 1024:16], e_kw)
+    wait(SC, e_kw)
+    e_kk = one(SC.activation(T.kk[:, 0:256], T.p5[:, 0:256], AF.Copy))
+
+    def landing(near_call):
+        return [[(r, len(en_)) for r in range(N) if r != rank for o, en_ in two_calls(T, topo, r, near_call)[c] if o == rank]
+                for c in range(2)]
+    qarr = [T.sem.qarr, sum(n for c in landing(0) for _, n in c), 0]
+    wait(V, qarr, e_qown)
+    v(V.tensor_scalar(T.tq[:], T.qr[:], 32767, None, A.bitwise_and))
+    v(V.tensor_scalar(T.ii[:], T.qr[:], 15, None, A.arith_shift_right))
+    vs()
+    e_th = one(V.tensor_copy(T.th[:], T.tq[:]))
+    e_il = one(V.tensor_copy(T.il[:], T.ii[:]))
+    wait(V, e_th)
+    e_tl = one(V.tensor_tensor(T.tl[:], T.tq[:], T.th[:], A.subtract))
+    wait(PE, e_u, e_th, e_tl)
+    for b in range(3):
+        for r in range(16):
+            u = T.uu[:, 128 * r:128 * r + 128]
+            o = T["p%d" % (2 + b)][:, r::16]
+            inc(PE.matmul(o, u, T.th[:, 32 * b:32 * b + 32], True, False), e_uw[b])
+            inc(PE.matmul(o, u, T.tl[:, 32 * b:32 * b + 32], False, True), e_uw[b])
+    e_tr, e_sg = [], ev()
+
+    def rep(b):
+        wait(SC, e_uw[b])
+        e_tr.append(one(SC.activation(T.trep[:, 512 * b:512 * b + 512], T["p%d" % (2 + b)][:], AF.Copy)))
+
+    def starts_of(h):
+        inc(SC.activation(T.sg[:, 768 * h:768 * h + 768], T.stwin[:, 0:272].indirect(T.il[:, 48 * h:48 * h + 48]), AF.Copy), e_sg)
+    wait(SC, e_il, e_stw, e_st256)
+    starts_of(0)
+    rep(0)
+    rep(1)
+    starts_of(1)
+    rep(2)
+    wait(PE, e_sg)
+    e_stq = wrap(T.p6[:, 0:96], lambda r: T.sg[:, r::16], ev())
+
+    wait(V, e_kl, e_pen, e_kk)
+    v(V.tensor_tensor(T.tt[:], T.kk[:, 0:272].indirect(T.kl[:, 0:48]), T.pen[:], A.add))
+    vs()
+    v(V.tensor_tensor(T.tt[:, 256:512], T.tt[:, 256:512], T.tt[:, 512:768], A.min))
+    wait(V, e_il)
+
+    def compare(out, w, a, b):
+        return V.tensor_tensor(out[:, a:b], T.tt[:, w:w + 256].indirect(T.il[:, a // 16:b // 16]), T.trep[:, a:b], A.is_le)
+
+    def count(out, a, ea, eb):
+        e = ev()
+        wait(PE, ea)
+        wrap(out, lambda r: T.ca[:, a + r:a + 768:16], e, True, False)
+        wait(PE, eb)
+        wrap(out, lambda r: T.cc[:, a + r:a + 768:16], e, False, True)
+        return e
+
+    def offsets(p, a, e):
+        c = slice(a, a + 48)
+        wait(V, e)
+        v(V.tensor_scalar(T.o1[:, c], p, 1.0, 8192.0, A.min, A.mult))
+        vs()
+        v(V.tensor_tensor(T.o2[:, c], T.o1[:, c], p, A.add))
+        vs()
+        v(V.tensor_tensor(T.o3[:, c], T.o2[:, c], T.p6[:, c], A.add))
+        vs()
+        return one(V.tensor_scalar(T.off[:, c], T.o3[:, c], float(F0 - 1 - 8192), 0.0, A.add, A.max))
+
+    ea0, eb0 = ev(), ev()
+    vs()
+    wait(V, e_tr[0])
+    inc(compare(T.ca, 0, 0, 512), ea0)
+    inc(compare(T.cc, 256, 0, 512), eb0)
+    wait(V, e_tr[1])
+    inc(compare(T.ca, 0, 512, 768), ea0)
+    inc(compare(T.cc, 256, 512, 768), eb0)
+    e_n0 = count(T.p0[:, 0:48], 0, ea0, eb0)
+    wait(V, e_tr[2])
+    ea1 = one(compare(T.ca, 0, 768, S))
+    wait(V, e_stq)
+    e_off0 = offsets(T.p0[:, 0:48], 0, e_n0)
+    eb1 = one(compare(T.cc, 256, 768, S))
+    e_n1 = count(T.p7[:, 0:48], 768, ea1, eb1)
+
+    calls = two_calls(T, topo, rank, 1)
+
+    def answers(c):
+        fused([([o], en_, T.ans[:, CAP * place(T, topo, rank, o):CAP * place(T, topo, rank, o) + CAP],
+                T.al[:, CAP * rank:CAP * rank + CAP]) for o, en_ in calls[c]], T.sem["aarr%d" % c])
+    wait(SC, e_off0, e_ff)
+    e_f0 = one(SC.activation(T.ans[:, 0:768], ffw.indirect(T.off[:, 0:48]), AF.Copy))
+    wait(g, e_f0)
+    answers(0)
+    wait(V, e_qs)
+    v(V.tensor_scalar(T.q8[:], T.qs[:], 12, None, A.arith_shift_right))
+    for q_ in (SC, V):
+        wait(q_, sarr, sarr2, e_sown)
+    for s in range(N - 1):
+        part = T.sl[:, I * order.index(s):I * order.index(s) + I]
+        inc(SC.activation(T.i1[:, s + 1::8], part, AF.Copy), e_i1)
+        v(V.tensor_scalar(T.i0[:, s + 1::8], part, 0.0, None, A.is_equal))
+    e_off1 = offsets(T.p7[:, 0:48], 48, e_n1)
+    wait(V, e_off1, e_ff)
+    e_f1 = ev()
+    inc(V.tensor_copy(T.ans[:, 768:960], ffw.indirect(T.off[:, 48:60])), e_f1)
+    wait(SC, e_off1)
+    inc(SC.activation(T.ans[:, 960:1344], ffw.indirect(T.off[:, 60:84]), AF.Copy), e_f1)
+    wait(g, e_f1)
+    answers(1)
+    e_aown = one(V.tensor_copy(T.al[:, CAP * rank:CAP * rank + CAP], ffw.indirect(T.off[:, 84:96])))
+
+    e_pidx = one(V.tensor_copy(T.pidx[:], T.q8[:]))
+    wait(V, e_i1)
+    e_p = one(V.tensor_tensor_scan(T.pp[:], T.i0[:], T.i1[:], 0.0, A.mult, A.add))
+    wait(SC, e_p, e_pidx)
+    wait(V, e_p, e_pidx)
+    ppw = T.pp[:, 0:8 * I]
+    e_pg = ev()
+    inc(SC.activation(T.d1[:, 0:S:2], ppw.indirect(T.pidx[:, 0:48]), AF.Copy), e_pg)
+    inc(V.tensor_copy(T.d1[:, S::2], ppw.indirect(T.pidx[:, 48:96])), e_pg)
+
+    e_o = ev()
+    wait(V, e_d0, e_aown)
+    wait(SC, e_aown)
+    for c, land in enumerate(landing(1)):
+        arr = [T.sem["aarr%d" % c], sum(n for _, n in land), 0]
+        parts = runs([r for r, _ in land] + ([rank] if c == 0 else []))
+        wait(SC, arr)
+        wait(V, arr)
+        e_c = []
+        for a, b in parts:
+            e_c.append(one(SC.activation(T.d1[:, 2 * CAP * a + 1:2 * CAP * b:2], T.al[:, CAP * a:CAP * b], AF.Copy)))
+            v(V.tensor_scalar(T.d0[:, 2 * CAP * a + 1:2 * CAP * b:2], T.al[:, CAP * a:CAP * b], 0.0, None, A.is_equal))
+        if c == 0:
+            wait(V, e_pg)
+        vs()
+        for (a, b), e in zip(parts, e_c):
+            w = slice(2 * CAP * a, 2 * CAP * b)
+            wait(V, e)
+            inc(V.tensor_tensor_scan(T.oo[:, w], T.d0[:, w], T.d1[:, w], 0.0, A.mult, A.add), e_o)
+
+    e_y = ev()
+    for q_, h in ((SC, 0), (V, 1)):
+        wait(q_, e_o, e_slot2)
+        half, lst = slice(512 * h, 512 * h + 512), T.oo[:, 0:2 * S].indirect(T.slot2[:, 32 * h:32 * h + 32])
+        e_yo = one(SC.activation(T.yo[:, half], lst, AF.Copy) if h == 0 else V.tensor_copy(T.yo[:, half], lst))
+        d_ = SC if h == 0 else SY
+        wait(d_, e_yo)
+        inc(d_.dma_start(T.y[:, half], T.yo[:, half]), e_y, 16)
+    wait(SY, e_y)
+    for e in evs + [sent]:
+        if e[1] > e[2]:
+            wait(g, e)

@@ -3,35 +3,39 @@ from concourse.mybir import AluOpType as A, ActivationFunctionType as AF
 
 N, M, I, Q, CAP = 8, 4096, 256, 1024, 192
 S = N * CAP
+C = S // 16
+B = CAP // 16
 BIG = 65536.0
-F0 = 16
-BF, F32, I32, U16 = "bfloat16", "float32", "int32", "uint16"
+BF, F16, F32, I32, U16 = "bfloat16", "float16", "float32", "int32", "uint16"
 
 SCRATCH = {}
 for _n, _w, _d in [
-    ("zero", 512, BF), ("b128", 128, BF), ("l2", 128, BF), ("zz", 144, BF), ("zf", 144, F32), ("uu", 2048, BF),
-    ("r0", 512, BF), ("m0", 512, BF), ("pen16", 352, BF), ("t16", 128, BF), ("pent", 352, BF), ("dump", 16, I32),
-    ("stb", 16, I32), ("tb", 256, I32), ("pm32", 256, I32), ("pm16", 256, U16),
-    ("qtin", 64, I32), ("sb", 32, BF), ("tc", 512, BF),
-    ("src", Q, I32), ("qwin", S, F32), ("stwin", 272, BF), ("twin", M, BF), ("tg", M, BF),
-    ("s1", 64, BF), ("sw", 64, BF), ("ee", 512, BF), ("cin", 512, BF), ("mx", 512, F32), ("a192", 64, F32),
-    ("slf", 64, F32), ("slot", 64, U16), ("slot2", 64, U16), ("qs", 96, I32), ("qr", 96, I32),
-    ("se", 32, I32), ("w1", 64, I32), ("w2", 64, I32), ("w3", 64, I32), ("w4", 32, I32),
-    ("kl", 48, U16), ("pl", 48, U16), ("offs", 16, U16), ("offr", 16, U16),
-    ("xw", M, BF), ("xs", M, BF), ("mk", M + 368, BF), ("ff", M + F0, BF),
+    ("zero", 512, BF), ("b128", 128, BF), ("l2", 128, BF), ("zz", 144, BF), ("zi", 144, BF), ("zt", 144, BF),
+    ("id8", 128, BF), ("uu", 2048, F16), ("r0", 512, BF), ("m0", 512, BF), ("pen16", 352, BF), ("t16", 128, BF),
+    ("pent", 352, BF), ("cq", C, BF),
+    ("tb", 256, I32), ("pm32", 256, I32), ("pm16", 256, U16),
+    ("qtin", 64, I32), ("qn", 144, I32), ("qp", 224, BF), ("tc", 512, BF),
+    ("src", Q, BF), ("qwin", S, BF), ("stwin", 272, BF), ("twin", M, BF), ("tg", M, BF),
+    ("s1", 64, BF), ("sw", 64, BF), ("ee", 512, BF), ("cin", 512, BF), ("mx", 512, F32),
+    ("slot", 64, U16), ("qs", 2 * C, F16), ("qr", 2 * C, F16),
+    ("se", 48, I32), ("w1", 80, I32), ("w2", 64, I32), ("w3", 32, I32),
+    ("kl", 48, U16), ("pl", 48, U16), ("ends", 32, U16),
+    ("xw", M, BF), ("xs", M, BF), ("mk", M + 368, BF), ("ff", M + 16, BF),
     ("pen", 768, BF), ("kk", 272, F32), ("tt", 768, F32),
-    ("ii", 96, I32), ("il", 96, U16), ("tq", 96, I32), ("th", 96, BF), ("tl", 96, BF),
-    ("trep", S, F32), ("ca", S, BF), ("cc", S, BF), ("sg", S, BF),
-    ("o1", 96, F32), ("o2", 96, F32), ("o3", 96, F32), ("off", 96, U16),
+    ("il", C, U16), ("trep", S, F32), ("sc", 2 * S, BF), ("cc", S, BF),
+    ("o1", C, F32), ("o2", C, F32), ("o3", C, F32), ("off", C, U16),
     ("ans", S, BF), ("al", S, BF), ("sl", 7 * I, BF), ("i0", 8 * I, BF), ("i1", 8 * I, BF), ("pp", 8 * I, BF),
-    ("q8", 96, I32), ("pidx", 96, U16),
-    ("d0", 2 * S, BF), ("d1", 2 * S, BF), ("oo", 2 * S, BF), ("yo", Q, BF),
+    ("pidx", 64, U16), ("d0", 2 * Q, BF), ("d1", 2 * Q, BF), ("oo", 2 * Q, BF), ("yo", Q, BF),
 ]:
     SCRATCH[_n] = ("sbuf", [128, _w], _d)
 for _k in range(8):
     SCRATCH["p%d" % _k] = ("psum", [128, 512], F32)
 
-SEMAPHORES = ["qarr", "sarr", "sarr2", "aarr0", "aarr1", "sent"] + ["e%d" % _k for _k in range(100)]
+SEMAPHORES = ["qarr0", "qarr1", "sarr", "sarr2", "aarr", "sent"] + ["e%d" % _k for _k in range(140)]
+
+OPT = {"xa": 2048, "ue": 2, "xsv": 1024, "relay": 1, "tfill": 2560, "groups": [2, 2, 4], "qcalls": [4, 2],
+       "tg0": 2048, "fill": 384,
+       "slv": 1, "ownv": 1, "cv": 256, "ansv": 192, "icv": 1, "sgv": 0, "penv": 0, "i1early": 1, "uw": 1536, "xfirst": 1}
 
 
 def peers(T, topo, r):
@@ -46,31 +50,35 @@ def bits(engines):
     return sum(1 << e for e in engines)
 
 
-def two_calls(T, topo, r, near_call):
+def engines_of(T, topo, r):
     c = T.cores
     far, near = peers(T, topo, r)
     off = topo.engines(c[r], c[far[0]])
-    on = [e for e in topo.engines(c[r], c[near[0]]) if e not in off]
-    q, h = len(off) // 4, len(off) // 2
-    calls = [[(far[k], off[k * q:(k + 1) * q]) for k in range(4)],
-             [(far[4 + k], off[k * h:(k + 1) * h]) for k in range(2)]]
-    calls[near_call].append((near[0], on))
-    return calls
+    return off, [e for e in topo.engines(c[r], c[near[0]]) if e not in off]
 
 
-def place(T, topo, o, r):
+def share(dests, engines):
+    n = len(dests)
+    return [(o, engines[k * len(engines) // n:(k + 1) * len(engines) // n]) for k, o in enumerate(dests)]
+
+
+def calls_of(T, topo, r, sizes, near_call, near_engines, back=False):
+    far, near = peers(T, topo, r)
+    if back:
+        far = blocks(T, topo, r)[:len(far)]
+    off, on = engines_of(T, topo, r)
+    first = [sum(sizes[:k]) for k in range(len(sizes) + 1)]
+    return [share(far[a:b], off) + (share(near, on[:near_engines]) if k == near_call else [])
+            for k, (a, b) in enumerate(zip(first, first[1:]))]
+
+
+def landing(T, topo, rank, *plan):
+    return sum(len(e) for r in range(N) for call in calls_of(T, topo, r, *plan) for o, e in call if o == rank)
+
+
+def blocks(T, topo, o):
     far, near = peers(T, topo, o)
-    return (far + near + [o]).index(r)
-
-
-def runs(blocks):
-    out = []
-    for b in sorted(blocks):
-        if out and out[-1][1] == b:
-            out[-1] = (out[-1][0], b + 1)
-        else:
-            out.append((b, b + 1))
-    return out
+    return sorted(far, key=lambda r: peers(T, topo, r)[0].index(o)) + near + [o]
 
 
 def rank_program(g, core, T, topo):
@@ -117,374 +125,434 @@ def rank_program(g, core, T, topo):
         g.remote_dma_fused([RemoteDMATransfer(dst_ids=[dst(o) for o in os_], dma_engine_mask=bits(en), remote_sem=sem,
                                               srcs=[s], dsts=[d] * len(os_)) for os_, en, s, d in items],
                            local_sem=sent[0])
-        sent[1] += sum(len(en) for _, en, _, _ in items)
+        sent[1] += sum(len(item[1]) for item in items)
 
     def wrap(out, rhs_of, e, first=True, last=True, z=T.zz):
         for r in range(16):
             inc(PE.matmul(out, z[:, 15 - r:143 - r], rhs_of(r), first and r == 0, last and r == 15), e)
         return e
 
-    far, near = peers(T, topo, rank)
+    def pick(q, out, win, lst):
+        return V.tensor_copy(out, win.indirect(lst)) if q is V else SC.activation(out, win.indirect(lst), AF.Copy)
 
-    e_st, e_qtin, e_tb, e_pm, e_x, e_src = ev(), ev(), ev(), ev(), ev(), ev()
+    def copy(q, out, in_):
+        return V.tensor_copy(out, in_) if q is V else SC.activation(out, in_, AF.Copy)
+
+    def cuts(a, b, n):
+        return [(k, min(k + n, b)) for k in range(a, b, n)]
+
+    far, near = peers(T, topo, rank)
+    off, on = engines_of(T, topo, rank)
+
+    e_qtin, e_qn, e_tb, e_pm, e_x = ev(), ev(), ev(), ev(), ev()
+    inc(SY.dma_start(T.tb[:], T.times[:]), e_tb, 16)
     for blk in range(2):
         for g2 in range(2):
             k = blk * 32 + g2 * 16
-            inc(SY.dma_start(T.qtin[:, k:k + 16], T.qt[g2::2, 512 * blk:512 * blk + 512]), e_qtin, 16)
-    inc(SY.dma_start(T.pm32[:], T.pm[:]), e_pm, 16)
-    inc(SY.dma_start(T.stb[:], T.starts[:, 0:I]), e_st, 16)
-    e_zero = one(V.memset(T.zero[:], 0.0))
-    e_s0 = one(V.memset(T.src[:], 0))
-    wait(SY, e_s0)
-    inc(SY.dma_start(T.src[0::16, :], T.qi[:]), e_src, 16)
-    inc(SY.dma_start(T.src[1::16, :], T.qt[:]), e_src, 16)
-    inc(SY.dma_start(T.xw[:], T.x[:]), e_x, 16)
-    inc(SY.dma_start(T.tb[:], T.times[:]), e_tb, 16)
+            inc((SY, SC)[g2].dma_start(T.qtin[:, k:k + 16], T.qt[g2::2, 512 * blk:512 * blk + 512]), e_qtin, 16)
+    inc(SY.dma_start(T.qn[:, 0:64], T.qt[:]), e_qn, 16)
+    inc(SC.dma_start(T.qn[:, 80:144], T.qi[:]), e_qn, 16)
+    inc(SC.dma_start(T.qn[:, 64:80], T.starts[:, 0:I]), e_qn, 16)
+    inc(SC.dma_start(T.pm32[:], T.pm[:]), e_pm, 16)
+    XA = OPT["xa"]
+    inc(SY.dma_start(T.xw[:, 0:XA], T.x[:, 0:XA]), e_x, 16)
 
-    e_z0, e_i1 = ev(), ev()
-    inc(V.memset(T.zz[:], 0.0), e_z0)
-    inc(V.memset(T.zf[:], 0.0), e_z0)
+    e_zero = one(V.memset(T.zero[:], 0.0))
+    e_z0 = ev()
+    for z in (T.zz, T.zi, T.zt):
+        inc(V.memset(z[:], 0.0), e_z0)
+    v(V.memset(T.m0[:], 1.0))
     e_w0 = one(V.memset(T.stwin[:, 0:I], 0.0))
     e_st256 = one(V.memset(T.stwin[:, I:272], float(M // 16)))
-    v(V.memset(T.r0[:], 1.0))
-    v(V.memset(T.m0[:], 1.0))
-    v(V.memset(T.kk[:, 256:272], 0.0))
-    v(V.memset(T.ff[:, 0:F0], 0.0))
-    v(V.memset(T.i0[:, 0::8], 0.0))
-    v(V.memset(T.i1[:, 0::8], 0.0))
     vs()
-    v(V.memset(T.r0[:, 0::64], 0.0))
     v(V.memset(T.m0[:, 0::8], 0.0))
+    e_tw0 = one(V.memset(T.twin[:, 0:OPT["tfill"]], 0.0))
 
+    def clear(ap, n):
+        return g.affine_select(ap, T.zero[:, 0:n], [[0, n]], A.is_ge, 0.0, 0, 0)
     wait(g, e_zero)
     blk16 = [[-16, 8], [0, 16]]
     inc(g.affine_select(T.b128[:], T.zero[:, 0:128], blk16, A.is_ge, 1.0, -16, 1), cg)
     inc(g.affine_select(T.l2[:], T.zero[:, 0:128], [[1, 128]], A.is_ge, -1.0, 0, -1), cg)
+    e_r0 = one(g.iota(T.r0[:], [[-B, N], [256, 64]], (N - 1) * B, 0, allow_small_or_imprecise_dtypes=True))
     wait(g, cg)
     e_b128 = one(g.affine_select(T.b128[:], T.b128[:], blk16, A.is_ge, 0.0, 0, 1))
     inc(g.affine_select(T.l2[:], T.l2[:], [[16, 8], [0, 16]], A.is_ge, 0.0, 15, -1), cg)
     wait(g, cg)
     e_l2 = one(g.affine_select(T.l2[:], T.l2[:], [[-1, 128]], A.not_equal, 2048.0, 0, 1))
+    wait(g, e_z0, e_b128)
+    e_z = ev()
+    inc(g.affine_select(T.zz[:, 15:143:16], T.b128[:, 0::16], [[0, 8]], A.is_ge, 0.0, 0, 0), e_z)
+    inc(g.affine_select(T.zi[:, 15:143:16], T.zero[:, 0:8], [[-16, 8]], A.not_equal, 1.0, 0, 1), e_z)
+    inc(g.affine_select(T.zt[:, 15:143:16], T.b128[:, 0::16], [[-16, 8]], A.not_equal, 0.0, 0, 1), e_z)
+    e_cq = one(g.iota(T.cq[:], [[-M // 16, N], [0, B]], -M // 32, 0, allow_small_or_imprecise_dtypes=True))
+    e_pad = ev()
+    inc(g.iota(T.se[:, 32:48], [[16, 16]], M, 1), e_pad)
+    inc(clear(T.ff[:, 0:1], 1), e_pad)
+    inc(clear(T.kk[:, 256:272], 16), e_pad)
     inc(g.affine_select(T.pen16[0:16, 0:272], T.zero[0:16, 0:272], [[-1, 16], [0, 17]], A.is_ge, BIG, 0, 1), cg)
     e_p16 = ev()
     inc(g.affine_select(T.pen16[0:16, 272:352], T.zero[0:16, 0:80], [[1, 80]], A.is_ge, BIG, -33, -1), e_p16)
     inc(g.affine_select(T.t16[0:16, :], T.zero[0:16, 0:128], [[0, 8], [-1, 16]], A.not_equal, 1.0, 0, 1), e_p16)
     wait(g, cg)
     inc(g.affine_select(T.pen16[0:16, 0:272], T.pen16[0:16, 0:272], [[0, 16], [1, 17]], A.is_ge, BIG, -1, -1), e_p16)
-    e_dump = one(g.iota(T.dump[:], [[16, 16]], M - 8192, 1))
-
-    wait(SC, e_zero)
-    e_qw0, e_tw0, e_d0 = ev(), ev(), ev()
-    for k in range(S // 512):
-        inc(SC.activation(T.qwin[:, 512 * k:512 * k + 512], T.zero[:], AF.Copy), e_qw0)
-    wait(SC, e_z0, e_b128)
-    e_z = one(SC.activation(T.zz[:, 15:143:16], T.b128[:, 0::16], AF.Copy))
-    e_zf0 = one(SC.activation(T.zf[:, 15:143:16], T.b128[:, 0::16], AF.Copy))
-    for k in range(M // 512):
-        inc(SC.activation(T.twin[:, 512 * k:512 * k + 512], T.zero[:], AF.Copy), e_tw0)
-    for k in range(S // 512):
-        inc(SC.activation(T.d0[:, 1024 * k:1024 * k + 1024:2], T.zero[:], AF.Copy), e_d0)
-    wait(g, e_zf0)
-    e_zf = one(g.affine_select(T.zf[:, 15:143:16], T.zf[:, 15:143:16], [[-16, 8]], A.not_equal, 32768.0, 0, 1))
     e_u = ev()
 
     def make_u(k):
         inc(g.affine_select(T.uu[:, 512 * k:512 * k + 512], T.zero[:], [[-1, 4], [-16, 8], [0, 16]],
                             A.not_equal, 1.0, -4 * k, 1), e_u)
-    for k in range(4):
+    for k in range(OPT["ue"]):
         make_u(k)
 
-    wait(V, e_qtin)
-    v(V.tensor_scalar(T.s1[:], T.qtin[:], 1.0 / 4096, 191.5 + 1.0 / 8192, A.mult, A.add))
-    vs()
-    v(V.transpose(T.sw[:], T.s1[:]))
-    vs()
-    e_e = ev()
-    for s in range(N):
-        inc(V.tensor_scalar(T.ee[:, 64 * s:64 * s + 64], T.sw[:], float(192 + s), None, A.is_equal), e_e)
-    wait(V, e_e)
-    e_cin = one(V.tensor_tensor_scan(T.cin[:], T.r0[:], T.ee[:], 0.0, A.mult, A.add))
-    wait(PE, e_b128, e_l2, e_e, e_cin)
-    e_d = ev()
-    for s in range(N):
-        inc(PE.matmul(T.p0[:, s::8], T.l2[:], T.ee[:, 64 * s:64 * s + 64], True, False), e_d)
-        inc(PE.matmul(T.p0[:, s::8], T.b128[:], T.cin[:, 64 * s:64 * s + 64], False, True), e_d)
-    v(V.tensor_scalar(T.a192[:], T.sw[:], float(CAP), -float(192 * CAP + 2049), A.mult, A.add))
-    wait(V, e_st)
-    e_c1 = one(V.tensor_copy(T.sb[:, 0:16], T.stb[:]))
-    wait(V, e_pm)
-    e_pm16 = one(V.tensor_copy(T.pm16[:], T.pm32[:]))
-    wait(V, e_c1)
-    e_c2 = one(V.tensor_tensor(T.sb[:, 16:32], T.stb[:], T.sb[:, 0:16], A.subtract))
-    wait(SY, e_w0, e_c1, e_c2)
-    e_stw = ev()
-    for k in range(2):
-        inc(SY.dma_start(T.stwin[k::16, 0:I], T.sb[:, 16 * k:16 * k + 16]), e_stw, 16)
-    wait(V, e_d)
-    v(V.tensor_tensor_scan(T.mx[:], T.m0[:], T.p0[:], 0.0, A.mult, A.max))
-    vs()
-    v(V.tensor_tensor(T.slf[:], T.mx[:, 7::8], T.a192[:], A.add))
-    vs()
-    e_slot = one(V.tensor_copy(T.slot[:], T.slf[:]))
-    wait(V, e_slot, e_src, e_qw0)
-    e_scat = one(V.tensor_copy(T.qwin[:, 0:S].indirect(T.slot[:, 0:64]), T.src[:]))
+    wait(SC, e_zero)
+    e_qw0, e_s0 = ev(), ev()
+    for a, b in cuts(0, Q, 512):
+        inc(copy(SC, T.src[:, a:b], T.zero[:]), e_s0)
+    for a, b in cuts(OPT["tfill"], M, 512):
+        inc(copy(SC, T.twin[:, a:b], T.zero[:, 0:b - a]), e_tw0)
+    for a, b in cuts(0, S, 512):
+        inc(copy(SC, T.qwin[:, a:b], T.zero[:]), e_qw0)
 
     wait(V, e_tb)
     e_t1 = one(V.tensor_copy(T.tc[:, 0:256], T.tb[:]))
-    e_slot2 = one(V.tensor_scalar(T.slot2[:], T.slf[:], 2.0, 1.0, A.mult, A.add))
+    wait(V, e_qtin)
+    e_s1 = one(V.tensor_scalar(T.s1[:], T.qtin[:], 1.0 / 4096, 191.5 + 1.0 / 8192, A.mult, A.add))
     wait(V, e_t1)
     e_t2 = one(V.tensor_tensor(T.tc[:, 256:512], T.tb[:], T.tc[:, 0:256], A.subtract))
     wait(SY, e_tw0, e_t1, e_t2)
     e_tw = ev()
     for k in range(2):
         inc(SY.dma_start(T.twin[k::16, :], T.tc[:, 256 * k:256 * k + 256]), e_tw, 16)
+    wait(V, e_qn)
+    e_hi = one(V.tensor_copy(T.qp[:, 0:144], T.qn[:]))
+    wait(V, e_s1)
+    e_sw = one(V.transpose(T.sw[:], T.s1[:]))
+    wait(V, e_hi)
+    e_lo = one(V.tensor_tensor(T.qp[:, 144:224], T.qn[:, 0:80], T.qp[:, 0:80], A.subtract))
+    wait(SY, e_s0, e_hi, e_lo)
+    e_src = ev()
+    for k, a in enumerate((80, 0, 144)):
+        inc(SY.dma_start(T.src[k::16, :], T.qp[:, a:a + 64]), e_src, 16)
+    wait(SY, e_w0)
+    e_stw = ev()
+    for k, a in enumerate((64, 208)):
+        inc(SY.dma_start(T.stwin[k::16, 0:I], T.qp[:, a:a + 16]), e_stw, 16)
+    if XA < M:
+        inc(SY.dma_start(T.xw[:, XA:M], T.x[:, XA:M]), e_x, 16)
 
-    wait(PE, e_p16)
-    e_pp = one(PE.matmul(T.p7[:, 0:352], T.t16[0:16, :], T.pen16[0:16, :], True, True))
+    wait(V, e_sw)
+    e_e = ev()
+    for k in range(N):
+        inc(V.tensor_scalar(T.ee[:, 64 * k:64 * k + 64], T.sw[:], float(192 + N - 1 - k), None, A.is_equal), e_e)
+    wait(V, e_e, e_r0)
+    e_cin = one(V.tensor_tensor_scan(T.cin[:], T.r0[:], T.ee[:], 1024.0, A.min, A.add))
+    wait(PE, e_b128, e_l2, e_e, e_cin)
+    e_d = ev()
+    for k in range(N):
+        inc(PE.matmul(T.p0[:, k::8], T.l2[:], T.ee[:, 64 * k:64 * k + 64], True, False), e_d)
+        inc(PE.matmul(T.p0[:, k::8], T.b128[:], T.cin[:, 64 * k:64 * k + 64], False, True), e_d)
+    wait(V, e_pm)
+    e_pm16 = one(V.tensor_copy(T.pm16[:], T.pm32[:]))
+    wait(V, e_d, cv)
+    v(V.tensor_tensor_scan(T.mx[:], T.m0[:], T.p0[:], 0.0, A.mult, A.max))
+    vs()
+    e_slot = one(V.tensor_scalar(T.slot[:], T.mx[:, 7::8], -2049.0, None, A.add))
+    wait(V, e_slot, e_src, e_qw0)
+    e_scat = one(V.tensor_copy(T.qwin[:, 0:S].indirect(T.slot[:, 0:64]), T.src[:]))
+
     wait(PE, e_z, e_stw, e_st256)
     e_se = ev()
     wrap(T.p6[:, 0:16], lambda r: T.stwin[:, r:I:16], e_se)
     wrap(T.p6[:, 16:32], lambda r: T.stwin[:, r + 1:I + 1:16], e_se)
-    wait(PE, e_scat, e_zf)
-    e_qwrap = wrap(T.p1[:, 0:96], lambda r: T.qwin[:, r::16], ev(), z=T.zf)
+    wait(PE, e_scat, e_cq)
+    e_qwrap = wrap(T.p1[:, 0:2 * C:2], lambda r: T.qwin[:, r::16], ev(), z=T.zi)
+    inc(PE.matmul(T.p1[:, 1:2 * C:2], T.b128[:], T.cq[:], True, False), e_qwrap)
+    wrap(T.p1[:, 1:2 * C:2], lambda r: T.qwin[:, r::16], e_qwrap, first=False, z=T.zt)
+    wait(PE, e_p16)
+    e_pp = one(PE.matmul(T.p7[:, 0:352], T.t16[0:16, :], T.pen16[0:16, :], True, True))
 
-    wait(SC, e_pp)
-    e_pent = one(SC.activation(T.pent[:], T.p7[:, 0:352], AF.Copy))
-    wait(SC, e_pm16, e_x)
-    e_xs = []
-    for k in range(4):
-        e_xs.append(one(SC.activation(T.xs[:, 1024 * k:1024 * k + 1024],
-                                      T.xw[:, 0:M].indirect(T.pm16[:, 64 * k:64 * k + 64]), AF.Copy)))
+    xw, tw = T.xw[:, 0:M], T.twin[:, 0:M]
+    e_xs, e_tg = [], []
+
+    def times_of(a, b):
+        wait(SC, e_tw, e_pm16)
+        e_tg.append((a, b, one(pick(SC, T.tg[:, a:b], tw, T.pm16[:, a // 16:b // 16]))))
+    for a, b in cuts(0, OPT["tg0"], 1024):
+        times_of(a, b)
+
+    def ticks_of(q, a, b):
+        wait(q, e_x, e_pm16)
+        e_xs.append((a, b, one(pick(q, T.xs[:, a:b], xw, T.pm16[:, a // 16:b // 16]))))
+    for a, b in cuts(0, M - OPT["xsv"], 1024):
+        ticks_of(SC, a, b)
+    nsc = len(e_xs)
+
+    def mask(k):
+        a, b, e = e_xs[k]
+        wait(V, e)
+        v(V.tensor_scalar(T.mk[:, a:b], T.xs[:, a:b], 0.0, None, A.is_equal))
 
     wait(V, e_se)
-    v(V.tensor_copy(T.se[:], T.p6[:, 0:32]))
-    vs()
+    v(V.tensor_copy(T.se[:, 0:32], T.p6[:, 0:32]))
+    if OPT["xsv"] and OPT["xfirst"]:
+        ticks_of(V, M - OPT["xsv"], M)
+    wait(V, cv, e_pad)
     st, en = T.se[:, 0:16], T.se[:, 16:32]
     v(V.tensor_scalar(T.w1[:, 0:16], st, 4, None, A.arith_shift_right))
     v(V.tensor_scalar(T.w1[:, 16:32], st, 15, None, A.bitwise_and))
     v(V.tensor_scalar(T.w1[:, 32:48], st, 0x1FF0, None, A.bitwise_and))
-    v(V.tensor_tensor(T.w1[:, 48:64], en, st, A.subtract))
+    v(V.tensor_tensor(T.w1[:, 48:64], en, st, A.not_equal))
+    v(V.tensor_tensor(T.w1[:, 64:80], en, st, A.is_equal))
+
+    wait(V, e_qwrap)
+    e_qs = one(V.tensor_copy(T.qs[:], T.p1[:, 0:2 * C]))
+    wait(SY, e_qs)
+    e_qown = one(SY.dma_start(T.qr[:, 14 * B:16 * B], T.qs[:, 2 * B * rank:2 * B * rank + 2 * B]), 16)
+    wait(g, e_qs)
+    for k, call in enumerate(calls_of(T, topo, rank, OPT["qcalls"], 1, 2)):
+        at = [2 * B * blocks(T, topo, o).index(rank) for o, _ in call]
+        fused([([o], e, T.qs[:, 2 * B * o:2 * B * o + 2 * B], T.qr[:, p:p + 2 * B]) for (o, e), p in zip(call, at)],
+              T.sem["qarr%d" % min(k, 1)])
+    qarr = [[T.sem.qarr0, len(off), 0], [T.sem.qarr1, len(off) * (len(OPT["qcalls"]) - 1) + 2, 0]]
+    e_id = one(g.affine_select(T.id8[:], T.zero[:, 0:128], [[-1, 128]], A.not_equal, 1.0 / N, 0, 1))
+    for k in range(OPT["ue"], 4):
+        make_u(k)
+
     vs()
     e_kl, e_pl = ev(), ev()
     for k, h in enumerate((1, 0, 2)):
         inc(V.tensor_scalar(T.kl[:, 16 * k:16 * k + 16], T.w1[:, 0:16], float(h), None, A.add), e_kl)
     v(V.tensor_tensor(T.w2[:, 0:16], en, T.w1[:, 32:48], A.subtract))
     v(V.tensor_scalar(T.w2[:, 16:32], T.w1[:, 16:32], 17.0, None, A.mult))
-    v(V.tensor_scalar(T.w2[:, 32:48], T.w1[:, 48:64], 1.0, 8192.0, A.min, A.mult))
+    v(V.tensor_tensor(T.w2[:, 32:64], T.w1[:, 48:80], T.se[:, 16:48], A.mult))
+    if OPT["xsv"] and not OPT["xfirst"]:
+        ticks_of(V, M - OPT["xsv"], M)
+    mask(0)
     vs()
     inc(V.tensor_scalar(T.pl[:, 0:16], T.w2[:, 0:16], 288.0, None, A.add), e_pl)
     inc(V.tensor_scalar(T.pl[:, 32:48], T.w2[:, 0:16], 272.0, None, A.add), e_pl)
     v(V.tensor_scalar(T.w3[:, 0:16], T.w2[:, 0:16], 16.0, None, A.min))
-    v(V.tensor_tensor(T.w3[:, 16:32], T.w2[:, 32:48], en, A.add))
-    v(V.tensor_tensor(T.w3[:, 32:48], st, T.w2[:, 32:48], A.subtract))
-    wait(V, e_dump)
+    v(V.tensor_tensor(T.w2[:, 48:64], T.w2[:, 48:64], st, A.max))
+    rest = list(range(nsc, len(e_xs))) + list(range(1, nsc))
+    mask(rest[0])
     vs()
-    v(V.tensor_tensor(T.w4[:, 0:16], T.w3[:, 0:16], T.w2[:, 16:32], A.add))
-    v(V.tensor_tensor(T.w4[:, 16:32], T.w3[:, 32:48], T.dump[:], A.min))
-    v(V.tensor_scalar(T.offs[:], T.w3[:, 16:32], float(F0 - 1 - 8192), 0.0, A.add, A.max))
-    vs()
-    inc(V.tensor_copy(T.pl[:, 16:32], T.w4[:, 0:16]), e_pl)
-    v(V.tensor_scalar(T.offr[:], T.w4[:, 16:32], 8192.0, None, A.add))
-
-    def mask(k):
-        wait(V, e_xs[k])
-        v(V.tensor_scalar(T.mk[:, 1024 * k:1024 * k + 1024], T.xs[:, 1024 * k:1024 * k + 1024], 0.0, None, A.is_equal))
-    mask(0)
-
-    wait(V, e_qwrap)
-    e_qs = one(V.tensor_copy(T.qs[:], T.p1[:, 0:96]))
-    e_qown = one(V.tensor_copy(T.qr[:, 84:96], T.p1[:, 12 * rank:12 * rank + 12]))
-    wait(g, e_qs)
-    for call in two_calls(T, topo, rank, 0):
-        fused([([o], en_, T.qs[:, 12 * o:12 * o + 12],
-                T.qr[:, 12 * place(T, topo, o, rank):12 * place(T, topo, o, rank) + 12]) for o, en_ in call], T.sem.qarr)
-
-    for k in range(1, 4):
+    v(V.tensor_tensor(T.w3[:, 16:32], T.w3[:, 0:16], T.w2[:, 16:32], A.add))
+    e_ends = one(V.tensor_copy(T.ends[:], T.w2[:, 32:64]))
+    for k in rest[1:]:
         mask(k)
+
+    wait(V, cv, e_ends)
+    v(V.tensor_copy(T.mk[:, 0:M + 368].indirect(T.ends[:, 16:32]), T.zero[:, 0:I]))
+    inc(V.tensor_copy(T.pl[:, 16:32], T.w3[:, 16:32]), e_pl)
     vs()
-    v(V.tensor_copy(T.mk[:, 0:M + 368].indirect(T.offr[:, 0:16]), T.zero[:, 0:I]))
-    vs()
-    e_ff = one(V.tensor_tensor_scan(T.ff[:, F0:F0 + M], T.mk[:, 0:M], T.xs[:], 0.0, A.mult, A.add))
-    ffw = T.ff[:, 0:F0 + M]
+    e_ff = one(V.tensor_tensor_scan(T.ff[:, 1:M + 1], T.mk[:, 0:M], T.xs[:], 0.0, A.mult, A.add))
+    ffw = T.ff[:, 0:M + 1]
     e_sown = ev()
     die = [topo.die(c) for c in T.cores]
     order = sorted(range(N - 1), key=lambda r: (die[r], r))
-    off = topo.engines(core, T.cores[far[0]])
-    if rank < N - 1:
-        mine = T.sl[:, I * order.index(rank):I * order.index(rank) + I]
-        wait(V, e_ff)
-        inc(V.tensor_copy(mine, ffw.indirect(T.offs[:, 0:16])), e_sown)
-        wait(g, e_sown)
-        fused([([o for o in far if die[o] == die[rank]], off, mine, mine)], T.sem.sarr)
-    same = [order.index(r) for r in order if die[r] == die[rank]]
-    sarr = [T.sem.sarr, len(off) * len([r for r in order if die[r] == die[rank] and r != rank]), 0]
-    wait(g, sarr)
-    block = T.sl[:, I * same[0]:I * same[-1] + I]
-    fused([(near, topo.engines(core, T.cores[near[0]]), block, block)], T.sem.sarr2)
-    sarr2 = [T.sem.sarr2, len(topo.engines(T.cores[near[0]], core)), 0]
 
-    wait(SC, e_tw)
-    e_tg = []
-    for k in range(3):
-        e_tg.append(one(SC.activation(T.tg[:, 1024 * k:1024 * k + 1024],
-                                      T.twin[:, 0:M].indirect(T.pm16[:, 64 * k:64 * k + 64]), AF.Copy)))
-        if k == 0:
-            wait(SC, e_pl, e_pent)
-            e_pen = one(SC.activation(T.pen[:], T.pent[:, 0:352].indirect(T.pl[:, 0:48]), AF.Copy))
-    wait(V, e_tw, e_pm16)
-    e_tg.append(one(V.tensor_copy(T.tg[:, 3072:M], T.twin[:, 0:M].indirect(T.pm16[:, 192:256]))))
-    e_kw, e_uw = ev(), [ev(), ev(), ev()]
-    for k in range(4):
-        wait(PE, e_tg[k])
-        wrap(T.p5[:, 64 * k:64 * k + 64], lambda r: T.tg[:, 1024 * k + r:1024 * k + 1024:16], e_kw)
+    def last_values(q):
+        if rank < N - 1:
+            mine = T.sl[:, I * order.index(rank):I * order.index(rank) + I]
+            wait(q, e_ff, e_ends, e_pad)
+            inc(pick(q, mine, ffw, T.ends[:, 0:16]), e_sown)
+            wait(g, e_sown)
+            fused([([o for o in far if die[o] == die[rank]], off, mine, mine)], T.sem.sarr)
+    if OPT["slv"]:
+        last_values(V)
+
+    e_kw = ev()
+    for n, (a, b) in enumerate(cuts(OPT["tg0"], M, 1024)):
+        times_of(a, b)
+        if n == 0:
+            wait(SC, e_pp)
+            e_pent = one(copy(SC, T.pent[:], T.p7[:, 0:352]))
+    for a, b, e in e_tg:
+        wait(PE, e)
+        wrap(T.p5[:, a // 16:b // 16], lambda r: T.tg[:, a + r:b:16], e_kw)
+    e_pen = ev()
+    for q, a, b in ((SC, 0, 768 - OPT["penv"]), (V, 768 - OPT["penv"], 768)):
+        if a < b:
+            wait(q, e_pl, e_pent)
+            inc(pick(q, T.pen[:, a:b], T.pent[:, 0:352], T.pl[:, a // 16:b // 16]), e_pen)
     wait(SC, e_kw)
-    e_kk = one(SC.activation(T.kk[:, 0:256], T.p5[:, 0:256], AF.Copy))
+    e_kk = one(SC.activation(T.kk[:, 0:256], T.p5[:, 0:256], AF.Identity, bias=-float(rank * M + M // 2)))
+    if not OPT["slv"]:
+        last_values(SC)
+    e_d0, e_i0 = ev(), ev()
+    inc(clear(T.i0[:, 0::8], I), e_i0)
+    inc(clear(T.i1[:, 0::8], I), e_i0)
+    for k in range(Q // 512):
+        inc(clear(T.d0[:, 1024 * k:1024 * k + 1024:2], 512), e_d0)
+    early = CAP * OPT["qcalls"][0]
+    banks = [(p, a, b) for p, (a, b) in zip((T.p2, T.p3, T.p4), cuts(0, S, 512))]
+    e_tr = []
 
-    def landing(near_call):
-        return [[(r, len(en_)) for r in range(N) if r != rank for o, en_ in two_calls(T, topo, r, near_call)[c] if o == rank]
-                for c in range(2)]
-    qarr = [T.sem.qarr, sum(n for c in landing(0) for _, n in c), 0]
-    wait(V, qarr, e_qown)
-    v(V.tensor_scalar(T.tq[:], T.qr[:], 32767, None, A.bitwise_and))
-    v(V.tensor_scalar(T.ii[:], T.qr[:], 15, None, A.arith_shift_right))
-    vs()
-    e_th = one(V.tensor_copy(T.th[:], T.tq[:]))
-    e_il = one(V.tensor_copy(T.il[:], T.ii[:]))
-    wait(V, e_th)
-    e_tl = one(V.tensor_tensor(T.tl[:], T.tq[:], T.th[:], A.subtract))
-    wait(PE, e_u, e_th, e_tl)
-    for b in range(3):
-        for r in range(16):
-            u = T.uu[:, 128 * r:128 * r + 128]
-            o = T["p%d" % (2 + b)][:, r::16]
-            inc(PE.matmul(o, u, T.th[:, 32 * b:32 * b + 32], True, False), e_uw[b])
-            inc(PE.matmul(o, u, T.tl[:, 32 * b:32 * b + 32], False, True), e_uw[b])
-    e_tr, e_sg = [], ev()
+    def unwrap(upto):
+        while len(e_tr) < len(banks) and banks[len(e_tr)][1] < upto:
+            p, a, b = banks[len(e_tr)]
+            wait(PE, e_u, qarr[0], *([] if b <= early else [qarr[1], e_qown]))
+            e_tr.append(ev())
+            for r in range(16):
+                inc(PE.matmul(p[:, r::16], T.uu[:, 128 * r:128 * r + 128], T.qr[:, a // 8 + 1:b // 8:2], True, True), e_tr[-1])
+    unwrap(OPT["uw"])
 
-    def rep(b):
-        wait(SC, e_uw[b])
-        e_tr.append(one(SC.activation(T.trep[:, 512 * b:512 * b + 512], T["p%d" % (2 + b)][:], AF.Copy)))
+    sizes = OPT["groups"]
+    K = len(sizes)
+    first = [CAP * sum(sizes[:k]) for k in range(K + 1)]
+    chunks = list(zip(first, first[1:]))
 
-    def starts_of(h):
-        inc(SC.activation(T.sg[:, 768 * h:768 * h + 768], T.stwin[:, 0:272].indirect(T.il[:, 48 * h:48 * h + 48]), AF.Copy), e_sg)
-    wait(SC, e_il, e_stw, e_st256)
-    starts_of(0)
-    rep(0)
-    rep(1)
-    starts_of(1)
-    rep(2)
-    wait(PE, e_sg)
-    e_stq = wrap(T.p6[:, 0:96], lambda r: T.sg[:, r::16], ev())
+    def pick_starts(q, k):
+        a, b = chunks[k]
+        wait(q, e_il[-1], e_stw, e_st256)
+        return one(pick(q, T.sc[:, 2 * a:a + b], T.stwin[:, 0:272], T.il[:, a // 16:b // 16]))
 
+    def instruments(k):
+        a, b = ((0, early), (early, S))[k]
+        wait(V, qarr[k], e_qown)
+        e_il.append(one(V.tensor_copy(T.il[:, a // 16:b // 16], T.qr[:, a // 8:b // 8:2])))
+    e_il = []
     wait(V, e_kl, e_pen, e_kk)
     v(V.tensor_tensor(T.tt[:], T.kk[:, 0:272].indirect(T.kl[:, 0:48]), T.pen[:], A.add))
+    instruments(0)
     vs()
     v(V.tensor_tensor(T.tt[:, 256:512], T.tt[:, 256:512], T.tt[:, 512:768], A.min))
-    wait(V, e_il)
 
-    def compare(out, w, a, b):
-        return V.tensor_tensor(out[:, a:b], T.tt[:, w:w + 256].indirect(T.il[:, a // 16:b // 16]), T.trep[:, a:b], A.is_le)
+    aplan = (sizes[:-1] + [sizes[-1] - 2], K - 1, len(on), True)
+    acalls = calls_of(T, topo, rank, *aplan)
+    cbank = (T.p0, T.p7, T.p5)
+    spread = []
 
-    def count(out, a, ea, eb):
-        e = ev()
-        wait(PE, ea)
-        wrap(out, lambda r: T.ca[:, a + r:a + 768:16], e, True, False)
-        wait(PE, eb)
-        wrap(out, lambda r: T.cc[:, a + r:a + 768:16], e, False, True)
-        return e
+    def times(k):
+        unwrap(chunks[k][1])
+        while len(spread) < len(banks) and banks[len(spread)][1] < chunks[k][1]:
+            p, a, b = banks[len(spread)]
+            wait(SC, e_tr[len(spread)])
+            spread.append(one(copy(SC, T.trep[:, a:b], p[:, 0:b - a])))
+        return list(spread)
 
-    def offsets(p, a, e):
-        c = slice(a, a + 48)
+    def compare(out, w, a, b, e):
+        return inc(V.tensor_tensor(out, T.tt[:, w:w + 256].indirect(T.il[:, a // 16:b // 16]), T.trep[:, a:b], A.is_le), e)
+
+    def offsets(k, e):
+        a, b = chunks[k]
+        n = (b - a) // 16
+        c, hits = slice(a // 16, b // 16), cbank[k][:, n:2 * n]
         wait(V, e)
-        v(V.tensor_scalar(T.o1[:, c], p, 1.0, 8192.0, A.min, A.mult))
+        v(V.tensor_copy(T.o2[:, c], cbank[k][:, 0:n]))
+        v(V.tensor_scalar(T.o1[:, c], hits, 8192.0, None, A.mult))
         vs()
-        v(V.tensor_tensor(T.o2[:, c], T.o1[:, c], p, A.add))
+        v(V.tensor_tensor(T.o2[:, c], T.o2[:, c], hits, A.add))
         vs()
-        v(V.tensor_tensor(T.o3[:, c], T.o2[:, c], T.p6[:, c], A.add))
+        v(V.tensor_tensor(T.o3[:, c], T.o1[:, c], T.o2[:, c], A.min))
         vs()
-        return one(V.tensor_scalar(T.off[:, c], T.o3[:, c], float(F0 - 1 - 8192), 0.0, A.add, A.max))
+        return one(V.tensor_copy(T.off[:, c], T.o3[:, c]))
 
-    ea0, eb0 = ev(), ev()
-    vs()
-    wait(V, e_tr[0])
-    inc(compare(T.ca, 0, 0, 512), ea0)
-    inc(compare(T.cc, 256, 0, 512), eb0)
-    wait(V, e_tr[1])
-    inc(compare(T.ca, 0, 512, 768), ea0)
-    inc(compare(T.cc, 256, 512, 768), eb0)
-    e_n0 = count(T.p0[:, 0:48], 0, ea0, eb0)
-    wait(V, e_tr[2])
-    ea1 = one(compare(T.ca, 0, 768, S))
-    wait(V, e_stq)
-    e_off0 = offsets(T.p0[:, 0:48], 0, e_n0)
-    eb1 = one(compare(T.cc, 256, 768, S))
-    e_n1 = count(T.p7[:, 0:48], 768, ea1, eb1)
+    sarr = [T.sem.sarr, len(off) * len([r for r in order if die[r] == die[rank] and r != rank]), 0]
+    sarr2 = [T.sem.sarr2, len(on), 0]
 
-    calls = two_calls(T, topo, rank, 1)
+    def relay():
+        same = [order.index(r) for r in order if die[r] == die[rank]]
+        wait(g, sarr)
+        block = T.sl[:, I * same[0]:I * same[-1] + I]
+        fused([(near, on, block, block)], T.sem.sarr2)
 
-    def answers(c):
-        fused([([o], en_, T.ans[:, CAP * place(T, topo, rank, o):CAP * place(T, topo, rank, o) + CAP],
-                T.al[:, CAP * rank:CAP * rank + CAP]) for o, en_ in calls[c]], T.sem["aarr%d" % c])
-    wait(SC, e_off0, e_ff)
-    e_f0 = one(SC.activation(T.ans[:, 0:768], ffw.indirect(T.off[:, 0:48]), AF.Copy))
-    wait(g, e_f0)
-    answers(0)
-    wait(V, e_qs)
-    v(V.tensor_scalar(T.q8[:], T.qs[:], 12, None, A.arith_shift_right))
-    for q_ in (SC, V):
-        wait(q_, sarr, sarr2, e_sown)
-    for s in range(N - 1):
-        part = T.sl[:, I * order.index(s):I * order.index(s) + I]
-        inc(SC.activation(T.i1[:, s + 1::8], part, AF.Copy), e_i1)
-        v(V.tensor_scalar(T.i0[:, s + 1::8], part, 0.0, None, A.is_equal))
-    e_off1 = offsets(T.p7[:, 0:48], 48, e_n1)
-    wait(V, e_off1, e_ff)
-    e_f1 = ev()
-    inc(V.tensor_copy(T.ans[:, 768:960], ffw.indirect(T.off[:, 48:60])), e_f1)
-    wait(SC, e_off1)
-    inc(SC.activation(T.ans[:, 960:1344], ffw.indirect(T.off[:, 60:84]), AF.Copy), e_f1)
-    wait(g, e_f1)
-    answers(1)
-    e_aown = one(V.tensor_copy(T.al[:, CAP * rank:CAP * rank + CAP], ffw.indirect(T.off[:, 84:96])))
+    def answers(k, e):
+        a, b = chunks[k]
+        b = min(b, S - CAP)
+        cut = b - OPT["ansv"] if k == K - 1 else b
+        e_a = ev()
+        for q, a_, b_ in ((SC, a, cut), (V, cut, b)):
+            if a_ < b_:
+                wait(q, e, e_ff, e_pad)
+                inc(pick(q, T.ans[:, a_:b_], ffw, T.off[:, a_ // 16:b_ // 16]), e_a)
+        if k == OPT["relay"]:
+            relay()
+        wait(g, e_a)
+        mine = blocks(T, topo, rank)
+        fused([([o], en_, T.ans[:, CAP * mine.index(o):CAP * mine.index(o) + CAP], T.al[:, CAP * rank:CAP * rank + CAP])
+               for o, en_ in acalls[k]], T.sem.aarr)
 
-    e_pidx = one(V.tensor_copy(T.pidx[:], T.q8[:]))
-    wait(V, e_i1)
+    e_i1 = ev()
+
+    def interleave(direct, queues):
+        for k, s in enumerate([s for s in order if (die[s] == die[rank]) == direct]):
+            part = T.sl[:, I * order.index(s):I * order.index(s) + I]
+            q = V if k < OPT["icv"] else SC
+            if q in queues:
+                wait(q, *((sarr, e_sown) if direct else (sarr2,)))
+                inc(copy(q, T.i1[:, s + 1::8], part), e_i1)
+            if V in queues:
+                wait(V, *((sarr, e_sown) if direct else (sarr2,)))
+                v(V.tensor_scalar(T.i0[:, s + 1::8], part, 0.0, None, A.is_equal))
+
+    wait(PE, e_kk, e_pent)
+    e_n = None
+    e_rep = times(0)
+    e_sg = pick_starts(SC, 0)
+    for k in range(K):
+        wait(V, e_il[-1], cv, *e_rep)
+        a, b = chunks[k]
+        n, mid = (b - a) // 16, min(b, a + OPT["fill"]) if k else b
+        ea = compare(T.sc[:, a + b:b + mid], 0, a, mid, ev())
+        if k == 0:
+            instruments(1)
+        e_off = offsets(k - 1, e_n) if k else None
+        if mid < b:
+            compare(T.sc[:, b + mid:2 * b], 0, mid, b, ea)
+        if k + 1 < K:
+            e_rep = times(k + 1)
+        if k:
+            answers(k - 1, e_off)
+        wait(PE, e_sg, ea)
+        e_n = wrap(cbank[k][:, 0:2 * n], lambda r: T.sc[:, 2 * a + r:2 * b:16], ev(), True, False)
+        if k + 1 < K:
+            e_sg = pick_starts(SC, k + 1)
+        wait(PE, compare(T.cc[:, a:b], 256, a, b, ev()))
+        wrap(cbank[k][:, n:2 * n], lambda r: T.cc[:, a + r:b:16], e_n, False, True)
+    wait(PE, e_id, e_qs)
+    e_qi = wrap(T.p1[:, 0:64], lambda r: T.src[:, r::16], ev(), last=False, z=T.zi)
+    inc(PE.matmul(T.p1[:, 0:64], T.id8[:], T.sw[:], False, True), e_qi)
+    if OPT["i1early"]:
+        interleave(True, [SC])
+    e_off = offsets(K - 1, e_n)
+    answers(K - 1, e_off)
+    if OPT["relay"] >= K:
+        relay()
+    qo = V if OPT["ownv"] else SC
+    wait(qo, e_off, e_ff)
+    e_aown = one(pick(qo, T.al[:, CAP * rank:CAP * rank + CAP], ffw, T.off[:, C - B:C]))
+
+    wait(V, e_qi)
+    e_pidx = one(V.tensor_scalar(T.pidx[:], T.p1[:, 0:64], float(N), -192.0, A.mult, A.add))
+    interleave(True, [V] if OPT["i1early"] else [V, SC])
+    interleave(False, [V, SC])
+    wait(V, e_i1, e_i0, cv)
     e_p = one(V.tensor_tensor_scan(T.pp[:], T.i0[:], T.i1[:], 0.0, A.mult, A.add))
-    wait(SC, e_p, e_pidx)
-    wait(V, e_p, e_pidx)
-    ppw = T.pp[:, 0:8 * I]
-    e_pg = ev()
-    inc(SC.activation(T.d1[:, 0:S:2], ppw.indirect(T.pidx[:, 0:48]), AF.Copy), e_pg)
-    inc(V.tensor_copy(T.d1[:, S::2], ppw.indirect(T.pidx[:, 48:96])), e_pg)
+    e_c = ev()
+    for q, a, b in ((V, 0, OPT["cv"]), (SC, OPT["cv"], Q)):
+        if a < b:
+            wait(q, e_p, e_pidx)
+            inc(pick(q, T.d1[:, 2 * a:2 * b:2], T.pp[:, 0:8 * I], T.pidx[:, a // 16:b // 16]), e_c)
 
-    e_o = ev()
-    wait(V, e_d0, e_aown)
-    wait(SC, e_aown)
-    for c, land in enumerate(landing(1)):
-        arr = [T.sem["aarr%d" % c], sum(n for _, n in land), 0]
-        parts = runs([r for r, _ in land] + ([rank] if c == 0 else []))
-        wait(SC, arr)
-        wait(V, arr)
-        e_c = []
-        for a, b in parts:
-            e_c.append(one(SC.activation(T.d1[:, 2 * CAP * a + 1:2 * CAP * b:2], T.al[:, CAP * a:CAP * b], AF.Copy)))
-            v(V.tensor_scalar(T.d0[:, 2 * CAP * a + 1:2 * CAP * b:2], T.al[:, CAP * a:CAP * b], 0.0, None, A.is_equal))
-        if c == 0:
-            wait(V, e_pg)
-        vs()
-        for (a, b), e in zip(parts, e_c):
-            w = slice(2 * CAP * a, 2 * CAP * b)
-            wait(V, e)
-            inc(V.tensor_tensor_scan(T.oo[:, w], T.d0[:, w], T.d1[:, w], 0.0, A.mult, A.add), e_o)
-
+    aarr = [T.sem.aarr, landing(T, topo, rank, *aplan), 0]
+    e_a = []
+    for h, q in enumerate((V, SC)):
+        wait(q, aarr, e_aown)
+        e_a.append(one(pick(q, T.d1[:, Q * h + 1:Q * h + Q:2], T.al[:, 0:S], T.slot[:, 32 * h:32 * h + 32])))
     e_y = ev()
-    for q_, h in ((SC, 0), (V, 1)):
-        wait(q_, e_o, e_slot2)
-        half, lst = slice(512 * h, 512 * h + 512), T.oo[:, 0:2 * S].indirect(T.slot2[:, 32 * h:32 * h + 32])
-        e_yo = one(SC.activation(T.yo[:, half], lst, AF.Copy) if h == 0 else V.tensor_copy(T.yo[:, half], lst))
-        d_ = SC if h == 0 else SY
-        wait(d_, e_yo)
-        inc(d_.dma_start(T.y[:, half], T.yo[:, half]), e_y, 16)
+    wait(V, e_d0)
+    for h in range(2):
+        w, odd, half = slice(Q * h, Q * h + Q), slice(Q * h + 1, Q * h + Q, 2), slice(512 * h, 512 * h + 512)
+        wait(V, e_a[h])
+        v(V.tensor_scalar(T.d0[:, odd], T.d1[:, odd], 0.0, None, A.is_equal))
+        wait(V, cv, e_c)
+        e_o = one(V.tensor_tensor_scan(T.oo[:, w], T.d0[:, w], T.d1[:, w], 0.0, A.mult, A.add))
+        q, d = ((SC, SC), (V, SY))[h]
+        wait(q, e_o)
+        e_yo = one(copy(q, T.yo[:, half], T.oo[:, odd]))
+        wait(d, e_yo)
+        inc(d.dma_start(T.y[:, half], T.yo[:, half]), e_y, 16)
     wait(SY, e_y)
     for e in evs + [sent]:
         if e[1] > e[2]:

@@ -11,18 +11,17 @@ BF, F16, F32, I32, U16 = "bfloat16", "float16", "float32", "int32", "uint16"
 SCRATCH = {}
 for _n, _w, _d in [
     ("zero", 512, BF), ("b128", 128, BF), ("l2", 128, BF), ("zz", 144, BF), ("zi", 144, BF), ("zt", 144, BF),
-    ("id8", 128, BF), ("uu", 2048, F16), ("r0", 512, BF), ("m0", 512, BF), ("pen16", 352, BF), ("t16", 128, BF),
-    ("pent", 352, BF), ("cq", C, BF),
-    ("tb", 256, I32), ("pm32", 256, I32), ("pm16", 256, U16),
-    ("qtin", 64, I32), ("qn", 144, I32), ("qp", 224, BF), ("tc", 512, BF),
+    ("id8", 128, BF), ("uu", 2048, F16), ("r0", 512, BF), ("m0", 512, BF), ("pent", 352, BF),
+    ("cq", C, BF),
+    ("tb", 272, I32), ("pm32", 256, I32), ("pm16", 256, U16),
+    ("qtin", 64, I32), ("qn", 128, I32), ("qp", 192, BF), ("tc", 544, BF),
     ("src", Q, BF), ("qwin", S, BF), ("stwin", 272, BF), ("twin", M, BF), ("tg", M, BF),
-    ("s1", 64, BF), ("sw", 64, BF), ("ee", 512, BF), ("cin", 512, BF), ("mx", 512, F32),
+    ("s1", 128, BF), ("sw", 128, BF), ("ee", 512, BF), ("cin", 512, BF), ("mx", 512, F32),
     ("slot", 64, U16), ("qs", 2 * C, F16), ("qr", 2 * C, F16),
-    ("se", 48, I32), ("w1", 80, I32), ("w2", 64, I32), ("w3", 32, I32),
-    ("kl", 48, U16), ("pl", 48, U16), ("ends", 32, U16),
+    ("se", 48, I32), ("w1", 80, I32), ("w2", 112, I32), ("li", 112, U16),
     ("xw", M, BF), ("xs", M, BF), ("mk", M + 368, BF), ("ff", M + 16, BF),
     ("pen", 768, BF), ("kk", 272, F32), ("tt", 768, F32),
-    ("il", C, U16), ("trep", S, F32), ("sc", 2 * S, BF), ("cc", S, BF),
+    ("il", C, U16), ("trep", S, F32), ("pre", 768, F32), ("sc", 2 * S, BF), ("cc", S, BF),
     ("o1", C, F32), ("o2", C, F32), ("o3", C, F32), ("off", C, U16),
     ("ans", S, BF), ("al", S, BF), ("sl", 7 * I, BF), ("i0", 8 * I, BF), ("i1", 8 * I, BF), ("pp", 8 * I, BF),
     ("pidx", 64, U16), ("d0", 2 * Q, BF), ("d1", 2 * Q, BF), ("oo", 2 * Q, BF), ("yo", Q, BF),
@@ -31,11 +30,12 @@ for _n, _w, _d in [
 for _k in range(8):
     SCRATCH["p%d" % _k] = ("psum", [128, 512], F32)
 
-SEMAPHORES = ["qarr0", "qarr1", "sarr", "sarr2", "aarr", "sent"] + ["e%d" % _k for _k in range(140)]
+SEMAPHORES = ["qarr0", "qarr1", "sarr", "sarr1", "sarr2", "aarr", "sent"] + ["e%d" % _k for _k in range(140)]
 
-OPT = {"xa": 2048, "ue": 2, "xsv": 1024, "relay": 1, "tfill": 2560, "groups": [2, 2, 4], "qcalls": [4, 2],
-       "tg0": 2048, "fill": 384,
-       "slv": 1, "ownv": 1, "cv": 256, "ansv": 192, "icv": 1, "sgv": 0, "penv": 0, "i1early": 1, "uw": 1536, "xfirst": 1}
+OPT = {"xa": 1536, "ue": 2, "xsv": 1024, "relay": 0, "tfill": 2560, "groups": [4, 4], "qcalls": [4, 2],
+       "tail": [0, 256, 640, 1024], "rep0": 0, "tat": 0, "xb": 1536, "xbat": 1, "tg0": 2048, "fill": 384,
+       "slv": 1, "ownv": 3, "cv": 512, "ansv": 384, "ic": ["SSS", "SS", "VSS"], "x0": 512, "f0": 2, "c0": 256, "ahead": 2, "piece": 128, "wide": 1,
+       "s1first": 0, "pmat": 1, "direct": 0, "i0": "S", "pre": 0, "ilfirst": 0, "align": 0, "ansv0": 0, "d0": 0, "xq": 512, "tgv": 0, "av": 1, "ysc": "GSV", "penv": 1, "i1early": [[1, 0], [1, 0]], "uw": 1536, "xfirst": 1024}
 
 
 def peers(T, topo, r):
@@ -101,10 +101,14 @@ def rank_program(g, core, T, topo):
     def one(ins, n=1):
         return inc(ins, ev(), n)
 
+    seen = [(q, []) for q in (g, V, SC, PE, SY)]
+
     def wait(q, *es):
+        mine = [s for k, s in seen if k is q][0]
         for e in es:
-            if e[1] > 0:
+            if e[1] > 0 and not [1 for f, n in mine if f is e and n == e[1]]:
                 q.wait_ge(e[0], e[1])
+                mine.append((e, e[1]))
                 e[2] = e[1]
 
     cv, cg = ev(), ev()
@@ -121,9 +125,9 @@ def rank_program(g, core, T, topo):
 
     sent = [T.sem.sent, 0, 0]
 
-    def fused(items, sem):
+    def fused(items):
         g.remote_dma_fused([RemoteDMATransfer(dst_ids=[dst(o) for o in os_], dma_engine_mask=bits(en), remote_sem=sem,
-                                              srcs=[s], dsts=[d] * len(os_)) for os_, en, s, d in items],
+                                              srcs=[s], dsts=ds) for os_, en, s, ds, sem in items],
                            local_sem=sent[0])
         sent[1] += sum(len(item[1]) for item in items)
 
@@ -145,14 +149,14 @@ def rank_program(g, core, T, topo):
     off, on = engines_of(T, topo, rank)
 
     e_qtin, e_qn, e_tb, e_pm, e_x = ev(), ev(), ev(), ev(), ev()
-    inc(SY.dma_start(T.tb[:], T.times[:]), e_tb, 16)
+    inc(SY.dma_start(T.qn[:, 0:64], T.qt[:]), e_qn, 16)
+    inc(SC.dma_start(T.qn[:, 64:128], T.qi[:]), e_qn, 16)
+    inc(SY.dma_start(T.tb[:, 0:256], T.times[:]), e_tb, 16)
+    inc(SC.dma_start(T.tb[:, 256:272], T.starts[:, 0:I]), e_tb, 16)
     for blk in range(2):
         for g2 in range(2):
             k = blk * 32 + g2 * 16
             inc((SY, SC)[g2].dma_start(T.qtin[:, k:k + 16], T.qt[g2::2, 512 * blk:512 * blk + 512]), e_qtin, 16)
-    inc(SY.dma_start(T.qn[:, 0:64], T.qt[:]), e_qn, 16)
-    inc(SC.dma_start(T.qn[:, 80:144], T.qi[:]), e_qn, 16)
-    inc(SC.dma_start(T.qn[:, 64:80], T.starts[:, 0:I]), e_qn, 16)
     inc(SC.dma_start(T.pm32[:], T.pm[:]), e_pm, 16)
     XA = OPT["xa"]
     inc(SY.dma_start(T.xw[:, 0:XA], T.x[:, 0:XA]), e_x, 16)
@@ -190,12 +194,11 @@ def rank_program(g, core, T, topo):
     inc(g.iota(T.se[:, 32:48], [[16, 16]], M, 1), e_pad)
     inc(clear(T.ff[:, 0:1], 1), e_pad)
     inc(clear(T.kk[:, 256:272], 16), e_pad)
-    inc(g.affine_select(T.pen16[0:16, 0:272], T.zero[0:16, 0:272], [[-1, 16], [0, 17]], A.is_ge, BIG, 0, 1), cg)
+    inc(g.affine_select(T.pent[0:16, 0:272], T.zero[0:16, 0:272], [[0, 17], [-1, 16]], A.is_ge, BIG, 0, 1), cg)
     e_p16 = ev()
-    inc(g.affine_select(T.pen16[0:16, 272:352], T.zero[0:16, 0:80], [[1, 80]], A.is_ge, BIG, -33, -1), e_p16)
-    inc(g.affine_select(T.t16[0:16, :], T.zero[0:16, 0:128], [[0, 8], [-1, 16]], A.not_equal, 1.0, 0, 1), e_p16)
+    inc(g.affine_select(T.pent[0:16, 272:352], T.zero[0:16, 0:80], [[1, 80]], A.is_ge, BIG, -33, -1), e_p16)
     wait(g, cg)
-    inc(g.affine_select(T.pen16[0:16, 0:272], T.pen16[0:16, 0:272], [[0, 16], [1, 17]], A.is_ge, BIG, -1, -1), e_p16)
+    inc(g.affine_select(T.pent[0:16, 0:272], T.pent[0:16, 0:272], [[1, 17], [0, 16]], A.is_ge, BIG, -1, -1), e_p16)
     e_u = ev()
 
     def make_u(k):
@@ -208,42 +211,56 @@ def rank_program(g, core, T, topo):
     e_qw0, e_s0 = ev(), ev()
     for a, b in cuts(0, Q, 512):
         inc(copy(SC, T.src[:, a:b], T.zero[:]), e_s0)
+    XB = OPT["xb"]
+    if OPT["xbat"] == 0 and XA < XB:
+        inc(SC.dma_start(T.xw[:, XA:XB], T.x[:, XA:XB]), e_x, 16)
     for a, b in cuts(OPT["tfill"], M, 512):
         inc(copy(SC, T.twin[:, a:b], T.zero[:, 0:b - a]), e_tw0)
+    if OPT["xbat"] == 1 and XA < XB:
+        inc(SC.dma_start(T.xw[:, XA:XB], T.x[:, XA:XB]), e_x, 16)
     for a, b in cuts(0, S, 512):
         inc(copy(SC, T.qwin[:, a:b], T.zero[:]), e_qw0)
+    e_i0 = ev()
 
-    wait(V, e_tb)
-    e_t1 = one(V.tensor_copy(T.tc[:, 0:256], T.tb[:]))
-    wait(V, e_qtin)
-    e_s1 = one(V.tensor_scalar(T.s1[:], T.qtin[:], 1.0 / 4096, 191.5 + 1.0 / 8192, A.mult, A.add))
-    wait(V, e_t1)
-    e_t2 = one(V.tensor_tensor(T.tc[:, 256:512], T.tb[:], T.tc[:, 0:256], A.subtract))
-    wait(SY, e_tw0, e_t1, e_t2)
     e_tw = ev()
-    for k in range(2):
-        inc(SY.dma_start(T.twin[k::16, :], T.tc[:, 256 * k:256 * k + 256]), e_tw, 16)
+
+    e_stw, e_src, e_s1 = ev(), ev(), ev()
     wait(V, e_qn)
-    e_hi = one(V.tensor_copy(T.qp[:, 0:144], T.qn[:]))
+    e_hi = one(V.tensor_copy(T.qp[:, 0:128], T.qn[:]))
+    wait(V, e_tb)
+    e_t1 = one(V.tensor_copy(T.tc[:, 0:272], T.tb[:]))
+    wait(V, e_hi)
+    e_lo = one(V.tensor_tensor(T.qp[:, 128:192], T.qn[:, 0:64], T.qp[:, 0:64], A.subtract))
+
+    def slices():
+        wait(V, e_qtin)
+        for k in range(2):
+            inc(V.tensor_scalar(T.s1[:, 64 * k:64 * k + 64], T.qtin[:], 1.0 / 4096, 191.5 + k + 1.0 / 8192, A.mult, A.add), e_s1)
+    slices()
+    wait(V, e_t1)
+    e_t2 = one(V.tensor_tensor(T.tc[:, 272:408], T.tb[:, 0:136], T.tc[:, 0:136], A.subtract))
     wait(V, e_s1)
     e_sw = one(V.transpose(T.sw[:], T.s1[:]))
-    wait(V, e_hi)
-    e_lo = one(V.tensor_tensor(T.qp[:, 144:224], T.qn[:, 0:80], T.qp[:, 0:80], A.subtract))
-    wait(SY, e_s0, e_hi, e_lo)
-    e_src = ev()
-    for k, a in enumerate((80, 0, 144)):
+    inc(V.tensor_tensor(T.tc[:, 408:544], T.tb[:, 136:272], T.tc[:, 136:272], A.subtract), e_t2)
+    wait(SY, e_s0, e_hi)
+    for k, a in enumerate((64, 0, 128)):
+        if k == 2:
+            wait(SY, e_lo)
         inc(SY.dma_start(T.src[k::16, :], T.qp[:, a:a + 64]), e_src, 16)
-    wait(SY, e_w0)
-    e_stw = ev()
-    for k, a in enumerate((64, 208)):
-        inc(SY.dma_start(T.stwin[k::16, 0:I], T.qp[:, a:a + 16]), e_stw, 16)
-    if XA < M:
-        inc(SY.dma_start(T.xw[:, XA:M], T.x[:, XA:M]), e_x, 16)
+    wait(SY, e_tw0, e_w0, e_t1, e_t2)
+    for k in range(2):
+        inc(SY.dma_start(T.twin[k::16, :], T.tc[:, 272 * k:272 * k + 256]), e_tw, 16)
+    for k in range(2):
+        inc(SY.dma_start(T.stwin[k::16, 0:I], T.tc[:, 272 * k + 256:272 * k + 272]), e_stw, 16)
+    if XB < M:
+        inc(SY.dma_start(T.xw[:, XB:M], T.x[:, XB:M]), e_x, 16)
 
     wait(V, e_sw)
     e_e = ev()
-    for k in range(N):
-        inc(V.tensor_scalar(T.ee[:, 64 * k:64 * k + 64], T.sw[:], float(192 + N - 1 - k), None, A.is_equal), e_e)
+    for k in range(0, N, 2):
+        inc(V.tensor_scalar(T.ee[:, 64 * k:64 * k + 128], T.sw[:], float(192 + N - 1 - k), None, A.is_equal), e_e)
+    wait(V, e_pm)
+    e_pm16 = one(V.tensor_copy(T.pm16[:], T.pm32[:]))
     wait(V, e_e, e_r0)
     e_cin = one(V.tensor_tensor_scan(T.cin[:], T.r0[:], T.ee[:], 1024.0, A.min, A.add))
     wait(PE, e_b128, e_l2, e_e, e_cin)
@@ -251,12 +268,19 @@ def rank_program(g, core, T, topo):
     for k in range(N):
         inc(PE.matmul(T.p0[:, k::8], T.l2[:], T.ee[:, 64 * k:64 * k + 64], True, False), e_d)
         inc(PE.matmul(T.p0[:, k::8], T.b128[:], T.cin[:, 64 * k:64 * k + 64], False, True), e_d)
-    wait(V, e_pm)
-    e_pm16 = one(V.tensor_copy(T.pm16[:], T.pm32[:]))
+    e_d0 = ev()
+    spare = [(T.d0[:, a:a + 512:2], e_d0) for a in range(0, 2 * Q, 512)] + [(T.i0[:, 0::8], e_i0), (T.i1[:, 0::8], e_i0)]
+
+    def fill(n=1):
+        for ap, e in [spare.pop(0) for _ in range(min(n, len(spare)))]:
+            inc(V.memset(ap, 0.0), e)
+    fill(OPT["f0"])
     wait(V, e_d, cv)
     v(V.tensor_tensor_scan(T.mx[:], T.m0[:], T.p0[:], 0.0, A.mult, A.max))
+    fill()
     vs()
     e_slot = one(V.tensor_scalar(T.slot[:], T.mx[:, 7::8], -2049.0, None, A.add))
+    fill()
     wait(V, e_slot, e_src, e_qw0)
     e_scat = one(V.tensor_copy(T.qwin[:, 0:S].indirect(T.slot[:, 0:64]), T.src[:]))
 
@@ -268,15 +292,17 @@ def rank_program(g, core, T, topo):
     e_qwrap = wrap(T.p1[:, 0:2 * C:2], lambda r: T.qwin[:, r::16], ev(), z=T.zi)
     inc(PE.matmul(T.p1[:, 1:2 * C:2], T.b128[:], T.cq[:], True, False), e_qwrap)
     wrap(T.p1[:, 1:2 * C:2], lambda r: T.qwin[:, r::16], e_qwrap, first=False, z=T.zt)
-    wait(PE, e_p16)
-    e_pp = one(PE.matmul(T.p7[:, 0:352], T.t16[0:16, :], T.pen16[0:16, :], True, True))
+    wait(SY, e_p16)
+    e_pent = ev()
+    for k in range(1, 8):
+        inc(SY.dma_start(T.pent[16 * k:16 * k + 16, :], T.pent[0:16, :]), e_pent, 16)
 
     xw, tw = T.xw[:, 0:M], T.twin[:, 0:M]
     e_xs, e_tg = [], []
 
-    def times_of(a, b):
-        wait(SC, e_tw, e_pm16)
-        e_tg.append((a, b, one(pick(SC, T.tg[:, a:b], tw, T.pm16[:, a // 16:b // 16]))))
+    def times_of(a, b, q=SC):
+        wait(q, e_tw, e_pm16)
+        e_tg.append((a, b, one(pick(q, T.tg[:, a:b], tw, T.pm16[:, a // 16:b // 16]))))
     for a, b in cuts(0, OPT["tg0"], 1024):
         times_of(a, b)
 
@@ -290,111 +316,141 @@ def rank_program(g, core, T, topo):
     def mask(k):
         a, b, e = e_xs[k]
         wait(V, e)
-        v(V.tensor_scalar(T.mk[:, a:b], T.xs[:, a:b], 0.0, None, A.is_equal))
+        inc(V.tensor_scalar(T.mk[:, a:b], T.xs[:, a:b], 0.0, None, A.is_equal), e_mk)
+    e_mk = ev()
 
     wait(V, e_se)
     v(V.tensor_copy(T.se[:, 0:32], T.p6[:, 0:32]))
-    if OPT["xsv"] and OPT["xfirst"]:
-        ticks_of(V, M - OPT["xsv"], M)
+    XV = M - OPT["xsv"]
+    ticks_of(V, XV, XV + OPT["x0"])
     wait(V, cv, e_pad)
     st, en = T.se[:, 0:16], T.se[:, 16:32]
-    v(V.tensor_scalar(T.w1[:, 0:16], st, 4, None, A.arith_shift_right))
-    v(V.tensor_scalar(T.w1[:, 16:32], st, 15, None, A.bitwise_and))
-    v(V.tensor_scalar(T.w1[:, 32:48], st, 0x1FF0, None, A.bitwise_and))
-    v(V.tensor_tensor(T.w1[:, 48:64], en, st, A.not_equal))
-    v(V.tensor_tensor(T.w1[:, 64:80], en, st, A.is_equal))
+    e_lists = ev()
+
+    def part(t, k, n=1):
+        return t[:, 16 * k:16 * (k + n)]
+
+    def lists(level):
+        vs()
+        if level == 0:
+            v(V.tensor_scalar(part(T.w1, 0), st, 0x1FF0, None, A.bitwise_and))
+            v(V.tensor_tensor(part(T.w1, 2), en, st, A.not_equal))
+            v(V.tensor_tensor(part(T.w1, 3), en, st, A.is_equal))
+            v(V.tensor_scalar(part(T.w2, 4), st, 4, None, A.arith_shift_right))
+            v(V.tensor_scalar(part(T.w1, 1), st, 15, None, A.bitwise_and))
+        if level == 1:
+            v(V.tensor_tensor(part(T.w2, 3), en, part(T.w1, 0), A.subtract))
+            v(V.tensor_tensor(part(T.w2, 0, 2), part(T.w1, 2, 2), T.se[:, 16:48], A.mult))
+            for k in (1, 2):
+                v(V.tensor_scalar(part(T.w2, 4 + k), part(T.w2, 4), float(k), None, A.add))
+        if level == 2:
+            v(V.tensor_scalar(part(T.w1, 4), part(T.w2, 3), 16.0, 16.0, A.min, A.mult))
+            v(V.tensor_tensor(part(T.w2, 1), part(T.w2, 1), st, A.max))
+        if level == 3:
+            v(V.tensor_tensor(part(T.w2, 2), part(T.w1, 4), part(T.w1, 1), A.add))
+        if level == 4:
+            inc(V.tensor_copy(T.li[:], T.w2[:]), e_lists)
+    lists(0)
+    ticks_of(V, XV + OPT["x0"], M)
 
     wait(V, e_qwrap)
     e_qs = one(V.tensor_copy(T.qs[:], T.p1[:, 0:2 * C]))
     wait(SY, e_qs)
     e_qown = one(SY.dma_start(T.qr[:, 14 * B:16 * B], T.qs[:, 2 * B * rank:2 * B * rank + 2 * B]), 16)
     wait(g, e_qs)
-    for k, call in enumerate(calls_of(T, topo, rank, OPT["qcalls"], 1, 2)):
+    qplan = (OPT["qcalls"], len(OPT["qcalls"]) - 1, 2)
+    for k, call in enumerate(calls_of(T, topo, rank, *qplan)):
         at = [2 * B * blocks(T, topo, o).index(rank) for o, _ in call]
-        fused([([o], e, T.qs[:, 2 * B * o:2 * B * o + 2 * B], T.qr[:, p:p + 2 * B]) for (o, e), p in zip(call, at)],
-              T.sem["qarr%d" % min(k, 1)])
-    qarr = [[T.sem.qarr0, len(off), 0], [T.sem.qarr1, len(off) * (len(OPT["qcalls"]) - 1) + 2, 0]]
-    e_id = one(g.affine_select(T.id8[:], T.zero[:, 0:128], [[-1, 128]], A.not_equal, 1.0 / N, 0, 1))
+        fused([([o], e, T.qs[:, 2 * B * o:2 * B * o + 2 * B], [T.qr[:, p:p + 2 * B]], T.sem["qarr%d" % min(k, 1)])
+               for (o, e), p in zip(call, at)])
+    q0 = len(off) if len(OPT["qcalls"]) > 1 else landing(T, topo, rank, *qplan)
+    qarr = [[T.sem.qarr0, q0, 0], [T.sem.qarr1, landing(T, topo, rank, *qplan) - q0, 0]]
     for k in range(OPT["ue"], 4):
         make_u(k)
+    e_id = one(g.affine_select(T.id8[:], T.zero[:, 0:128], [[-1, 128]], A.not_equal, 1.0 / N, 0, 1))
 
-    vs()
-    e_kl, e_pl = ev(), ev()
-    for k, h in enumerate((1, 0, 2)):
-        inc(V.tensor_scalar(T.kl[:, 16 * k:16 * k + 16], T.w1[:, 0:16], float(h), None, A.add), e_kl)
-    v(V.tensor_tensor(T.w2[:, 0:16], en, T.w1[:, 32:48], A.subtract))
-    v(V.tensor_scalar(T.w2[:, 16:32], T.w1[:, 16:32], 17.0, None, A.mult))
-    v(V.tensor_tensor(T.w2[:, 32:64], T.w1[:, 48:80], T.se[:, 16:48], A.mult))
-    if OPT["xsv"] and not OPT["xfirst"]:
-        ticks_of(V, M - OPT["xsv"], M)
-    mask(0)
-    vs()
-    inc(V.tensor_scalar(T.pl[:, 0:16], T.w2[:, 0:16], 288.0, None, A.add), e_pl)
-    inc(V.tensor_scalar(T.pl[:, 32:48], T.w2[:, 0:16], 272.0, None, A.add), e_pl)
-    v(V.tensor_scalar(T.w3[:, 0:16], T.w2[:, 0:16], 16.0, None, A.min))
-    v(V.tensor_tensor(T.w2[:, 48:64], T.w2[:, 48:64], st, A.max))
-    rest = list(range(nsc, len(e_xs))) + list(range(1, nsc))
-    mask(rest[0])
-    vs()
-    v(V.tensor_tensor(T.w3[:, 16:32], T.w3[:, 0:16], T.w2[:, 16:32], A.add))
-    e_ends = one(V.tensor_copy(T.ends[:], T.w2[:, 32:64]))
-    for k in rest[1:]:
+    rest = list(range(nsc, len(e_xs))) + list(range(nsc))
+    for level in range(1, 5):
+        lists(level)
+        mask(rest.pop(0))
+    for k in rest:
         mask(k)
 
-    wait(V, cv, e_ends)
-    v(V.tensor_copy(T.mk[:, 0:M + 368].indirect(T.ends[:, 16:32]), T.zero[:, 0:I]))
-    inc(V.tensor_copy(T.pl[:, 16:32], T.w3[:, 16:32]), e_pl)
+    e_pen = ev()
+    pens = [(k, a, lst) for k, (a, lst) in enumerate(((0, 2), (288, 3), (272, 3)))]
+
+    def penalty(q):
+        k, a, lst = pens.pop()
+        wait(q, e_lists, e_pent, e_p16)
+        inc(pick(q, T.pen[:, I * k:I * k + I], T.pent[:, a:352], part(T.li, lst)), e_pen)
+    if OPT["penv"] > 0:
+        penalty(V)
+    else:
+        fill()
+    wait(V, e_mk, e_lists)
+    v(V.tensor_copy(T.mk[:, 0:M + 368].indirect(part(T.li, 1)), T.zero[:, 0:I]))
+    if OPT["penv"] > 1:
+        penalty(V)
+    else:
+        fill()
     vs()
     e_ff = one(V.tensor_tensor_scan(T.ff[:, 1:M + 1], T.mk[:, 0:M], T.xs[:], 0.0, A.mult, A.add))
+    fill()
     ffw = T.ff[:, 0:M + 1]
     e_sown = ev()
     die = [topo.die(c) for c in T.cores]
-    order = sorted(range(N - 1), key=lambda r: (die[r], r))
+
+    def held(r):
+        far_, near_ = peers(T, topo, r)
+        parts = ([s for s in far_ if die[s] == die[r]], [r] + near_, [s for s in far_ if die[s] != die[r]])
+        if OPT["direct"]:
+            parts = ([], [r] + near_, far_)
+        return [[s for s in p if s < N - 1] for p in parts]
+
+    def column(r, s):
+        return I * sum(held(r), []).index(s)
+
+    def lasts(r, slices):
+        return T.sl[:, column(r, slices[0]):column(r, slices[0]) + I * len(slices)]
 
     def last_values(q):
         if rank < N - 1:
-            mine = T.sl[:, I * order.index(rank):I * order.index(rank) + I]
-            wait(q, e_ff, e_ends, e_pad)
-            inc(pick(q, mine, ffw, T.ends[:, 0:16]), e_sown)
+            mine = lasts(rank, [rank])
+            wait(q, e_ff, e_lists, e_pad)
+            inc(pick(q, mine, ffw, part(T.li, 0)), e_sown)
             wait(g, e_sown)
-            fused([([o for o in far if die[o] == die[rank]], off, mine, mine)], T.sem.sarr)
+            to = [o for o in far if die[o] == die[rank] or OPT["direct"]]
+            fused([(to, off, mine, [lasts(o, [rank]) for o in to], T.sem.sarr2 if OPT["direct"] else T.sem.sarr),
+                   (near, on, mine, [lasts(near[0], [rank])], T.sem.sarr1)])
     if OPT["slv"]:
         last_values(V)
 
     e_kw = ev()
-    for n, (a, b) in enumerate(cuts(OPT["tg0"], M, 1024)):
+    for a, b in cuts(OPT["tg0"], M - OPT["tgv"], 1024):
         times_of(a, b)
-        if n == 0:
-            wait(SC, e_pp)
-            e_pent = one(copy(SC, T.pent[:], T.p7[:, 0:352]))
+    if OPT["tgv"]:
+        times_of(M - OPT["tgv"], M, V)
     for a, b, e in e_tg:
         wait(PE, e)
         wrap(T.p5[:, a // 16:b // 16], lambda r: T.tg[:, a + r:b:16], e_kw)
-    e_pen = ev()
-    for q, a, b in ((SC, 0, 768 - OPT["penv"]), (V, 768 - OPT["penv"], 768)):
-        if a < b:
-            wait(q, e_pl, e_pent)
-            inc(pick(q, T.pen[:, a:b], T.pent[:, 0:352], T.pl[:, a // 16:b // 16]), e_pen)
+    while pens:
+        penalty(SC)
     wait(SC, e_kw)
     e_kk = one(SC.activation(T.kk[:, 0:256], T.p5[:, 0:256], AF.Identity, bias=-float(rank * M + M // 2)))
     if not OPT["slv"]:
         last_values(SC)
-    e_d0, e_i0 = ev(), ev()
-    inc(clear(T.i0[:, 0::8], I), e_i0)
-    inc(clear(T.i1[:, 0::8], I), e_i0)
-    for k in range(Q // 512):
-        inc(clear(T.d0[:, 1024 * k:1024 * k + 1024:2], 512), e_d0)
-    early = CAP * OPT["qcalls"][0]
-    banks = [(p, a, b) for p, (a, b) in zip((T.p2, T.p3, T.p4), cuts(0, S, 512))]
+    early = CAP * OPT["qcalls"][0] if len(OPT["qcalls"]) > 1 else S - 16
+    banks = [(p, a, b) for p, (a, b) in zip((T.p2, T.p3, T.p4, T.p6),
+                                            cuts(0, early, 512) + cuts(early, S, 512) if OPT["align"] else cuts(0, S, 512))]
     e_tr = []
 
     def unwrap(upto):
         while len(e_tr) < len(banks) and banks[len(e_tr)][1] < upto:
             p, a, b = banks[len(e_tr)]
-            wait(PE, e_u, qarr[0], *([] if b <= early else [qarr[1], e_qown]))
+            wait(PE, e_u, e_lists, qarr[0], *([] if b <= early else [qarr[1], e_qown]))
             e_tr.append(ev())
             for r in range(16):
-                inc(PE.matmul(p[:, r::16], T.uu[:, 128 * r:128 * r + 128], T.qr[:, a // 8 + 1:b // 8:2], True, True), e_tr[-1])
+                inc(PE.matmul(p[:, r:b - a:16], T.uu[:, 128 * r:128 * r + 128], T.qr[:, a // 8 + 1:b // 8:2], True, True), e_tr[-1])
     unwrap(OPT["uw"])
 
     sizes = OPT["groups"]
@@ -412,11 +468,15 @@ def rank_program(g, core, T, topo):
         wait(V, qarr[k], e_qown)
         e_il.append(one(V.tensor_copy(T.il[:, a // 16:b // 16], T.qr[:, a // 8:b // 8:2])))
     e_il = []
-    wait(V, e_kl, e_pen, e_kk)
-    v(V.tensor_tensor(T.tt[:], T.kk[:, 0:272].indirect(T.kl[:, 0:48]), T.pen[:], A.add))
-    instruments(0)
+    if OPT["ilfirst"]:
+        instruments(0)
+    wait(V, e_lists, e_pen, e_kk)
+    v(V.tensor_tensor(T.tt[:], T.kk[:, 0:272].indirect(part(T.li, 4, 3)), T.pen[:], A.add))
+    if not OPT["ilfirst"]:
+        instruments(0)
+    fill(9)
     vs()
-    v(V.tensor_tensor(T.tt[:, 256:512], T.tt[:, 256:512], T.tt[:, 512:768], A.min))
+    v(V.tensor_tensor(T.tt[:, 0:256], T.tt[:, 0:256], T.tt[:, 512:768], A.min))
 
     aplan = (sizes[:-1] + [sizes[-1] - 2], K - 1, len(on), True)
     acalls = calls_of(T, topo, rank, *aplan)
@@ -434,33 +494,58 @@ def rank_program(g, core, T, topo):
     def compare(out, w, a, b, e):
         return inc(V.tensor_tensor(out, T.tt[:, w:w + 256].indirect(T.il[:, a // 16:b // 16]), T.trep[:, a:b], A.is_le), e)
 
-    def offsets(k, e):
+    def offsets(k, e, between):
         a, b = chunks[k]
         n = (b - a) // 16
-        c, hits = slice(a // 16, b // 16), cbank[k][:, n:2 * n]
-        wait(V, e)
-        v(V.tensor_copy(T.o2[:, c], cbank[k][:, 0:n]))
-        v(V.tensor_scalar(T.o1[:, c], hits, 8192.0, None, A.mult))
-        vs()
-        v(V.tensor_tensor(T.o2[:, c], T.o2[:, c], hits, A.add))
-        vs()
-        v(V.tensor_tensor(T.o3[:, c], T.o1[:, c], T.o2[:, c], A.min))
-        vs()
-        return one(V.tensor_copy(T.off[:, c], T.o3[:, c]))
+        c = slice(a // 16, b // 16)
+        steps = (lambda: V.tensor_scalar(T.o1[:, c], cbank[k][:, n:2 * n], 8192.0, None, A.mult),
+                 lambda: V.tensor_tensor(T.o2[:, c], T.o1[:, c], cbank[k][:, 0:n], A.min),
+                 lambda: V.tensor_tensor(T.o3[:, c], T.o2[:, c], cbank[k][:, n:2 * n], A.add),
+                 lambda: V.tensor_copy(T.off[:, c], T.o3[:, c]))
+        for step in steps:
+            if between:
+                between.pop(0)()
+            wait(V, e)
+            e = one(step())
+        return e
 
-    sarr = [T.sem.sarr, len(off) * len([r for r in order if die[r] == die[rank] and r != rank]), 0]
-    sarr2 = [T.sem.sarr2, len(on), 0]
+    sarr = [T.sem.sarr, len(off) * len(held(rank)[0]), 0]
+    sarr1 = [T.sem.sarr1, len(on) * (near[0] < N - 1), 0]
+    wide = off + on if OPT["wide"] else on
+    sarr2 = [T.sem.sarr2, len(off) * len(held(rank)[2]) if OPT["direct"] else len(wide), 0]
 
     def relay():
-        same = [order.index(r) for r in order if die[r] == die[rank]]
+        if OPT["direct"]:
+            return
         wait(g, sarr)
-        block = T.sl[:, I * same[0]:I * same[-1] + I]
-        fused([(near, on, block, block)], T.sem.sarr2)
+        fused([(near, wide, lasts(rank, held(rank)[0]), [lasts(near[0], held(rank)[0])], T.sem.sarr2)])
+        interleave(0, g)
+
+    e_i1 = ev()
+
+    def interleave(part, q):
+        for s, who in zip(held(rank)[part], OPT["ic"][part]):
+            came = ((sarr,), (sarr1, e_sown), (sarr2,))[part]
+            if q is {"G": g, "S": SC, "V": V}[who]:
+                wait(q, *came)
+                if q is g:
+                    inc(g.affine_select(T.i1[:, s + 1::8], lasts(rank, [s]), [[0, I]], A.is_ge, 0.0, 0, 0), e_i1)
+                else:
+                    inc(copy(q, T.i1[:, s + 1::8], lasts(rank, [s])), e_i1)
+            if q is V and s not in marked:
+                mark(part, s)
+
+    marked = []
+
+    def mark(part, s):
+        marked.append(s)
+        wait(V, *((sarr,), (sarr1, e_sown), (sarr2,))[part])
+        inc(V.tensor_scalar(T.i0[:, s + 1::8], lasts(rank, [s]), 0.0, None, A.is_equal), e_i1)
 
     def answers(k, e):
         a, b = chunks[k]
         b = min(b, S - CAP)
-        cut = b - OPT["ansv"] if k == K - 1 else b
+        cut = b - (OPT["ansv"] if k == K - 1 else OPT["ansv0"])
         e_a = ev()
         for q, a_, b_ in ((SC, a, cut), (V, cut, b)):
             if a_ < b_:
@@ -470,65 +555,76 @@ def rank_program(g, core, T, topo):
             relay()
         wait(g, e_a)
         mine = blocks(T, topo, rank)
-        fused([([o], en_, T.ans[:, CAP * mine.index(o):CAP * mine.index(o) + CAP], T.al[:, CAP * rank:CAP * rank + CAP])
-               for o, en_ in acalls[k]], T.sem.aarr)
+        fused([([o], en_, T.ans[:, CAP * mine.index(o):CAP * mine.index(o) + CAP],
+                [T.al[:, CAP * rank:CAP * rank + CAP]], T.sem.aarr) for o, en_ in acalls[k]])
 
-    e_i1 = ev()
-
-    def interleave(direct, queues):
-        for k, s in enumerate([s for s in order if (die[s] == die[rank]) == direct]):
-            part = T.sl[:, I * order.index(s):I * order.index(s) + I]
-            q = V if k < OPT["icv"] else SC
-            if q in queues:
-                wait(q, *((sarr, e_sown) if direct else (sarr2,)))
-                inc(copy(q, T.i1[:, s + 1::8], part), e_i1)
-            if V in queues:
-                wait(V, *((sarr, e_sown) if direct else (sarr2,)))
-                v(V.tensor_scalar(T.i0[:, s + 1::8], part, 0.0, None, A.is_equal))
-
-    wait(PE, e_kk, e_pent)
+    interleave(1, g)
+    wait(PE, e_id, e_qs)
+    e_qi = wrap(T.p1[:, 0:64], lambda r: T.src[:, r::16], ev(), last=False, z=T.zi)
+    inc(PE.matmul(T.p1[:, 0:64], T.id8[:], T.sw[:, 0:64], False, True), e_qi)
+    wait(PE, e_kk)
     e_n = None
     e_rep = times(0)
+    times(OPT["rep0"])
     e_sg = pick_starts(SC, 0)
     for k in range(K):
-        wait(V, e_il[-1], cv, *e_rep)
+        wait(V, e_il[-1], *e_rep)
         a, b = chunks[k]
+        eb, a2 = ev(), a + (0 if k else OPT["c0"])
+        if a < a2:
+            compare(T.cc[:, a:a2], 256, a, a2, eb)
+        vs()
         n, mid = (b - a) // 16, min(b, a + OPT["fill"]) if k else b
         ea = compare(T.sc[:, a + b:b + mid], 0, a, mid, ev())
         if k == 0:
             instruments(1)
-        e_off = offsets(k - 1, e_n) if k else None
-        if mid < b:
+        rest_ = [lambda lo=lo, hi=hi: compare(T.sc[:, b + lo:b + hi], 0, lo, hi, ea) for lo, hi in cuts(mid, b, OPT["piece"])]
+        e_off = offsets(k - 1, e_n, [lambda: None] + rest_ if OPT["piece"] < 384 else []) if k else None
+        if OPT["piece"] >= 384 and mid < b:
             compare(T.sc[:, b + mid:2 * b], 0, mid, b, ea)
         if k + 1 < K:
             e_rep = times(k + 1)
         if k:
             answers(k - 1, e_off)
         wait(PE, e_sg, ea)
-        e_n = wrap(cbank[k][:, 0:2 * n], lambda r: T.sc[:, 2 * a + r:2 * b:16], ev(), True, False)
+        e_st = wrap(cbank[k][:, 0:2 * n], lambda r: T.sc[:, 2 * a + r:2 * b:16], ev(), True, False)
         if k + 1 < K:
             e_sg = pick_starts(SC, k + 1)
-        wait(PE, compare(T.cc[:, a:b], 256, a, b, ev()))
-        wrap(cbank[k][:, n:2 * n], lambda r: T.cc[:, a + r:b:16], e_n, False, True)
-    wait(PE, e_id, e_qs)
-    e_qi = wrap(T.p1[:, 0:64], lambda r: T.src[:, r::16], ev(), last=False, z=T.zi)
-    inc(PE.matmul(T.p1[:, 0:64], T.id8[:], T.sw[:], False, True), e_qi)
-    if OPT["i1early"]:
-        interleave(True, [SC])
-    e_off = offsets(K - 1, e_n)
+        wait(PE, compare(T.cc[:, a2:b], 256, a2, b, eb))
+        e_n = wrap(cbank[k][:, 0:n], lambda r: T.cc[:, a + r:b:16], e_st, False, True)
+    for k in OPT["i1early"][0]:
+        interleave(k, SC)
+    marks = [lambda k=k, s=s: mark(k, s) for k in OPT["i1early"][1] for s in held(rank)[k]]
+    wait(V, e_qi)
+    marks.append(lambda: inc(V.tensor_scalar(T.pidx[:], T.p1[:, 0:64], float(N), -192.0, A.mult, A.add), e_pidx))
+    e_pidx = ev()
+    while len(marks) > 5:
+        marks.pop(0)()
+    e_off = offsets(K - 1, e_n, marks)
+    while marks:
+        marks.pop(0)()
     answers(K - 1, e_off)
     if OPT["relay"] >= K:
         relay()
-    qo = V if OPT["ownv"] else SC
-    wait(qo, e_off, e_ff)
-    e_aown = one(pick(qo, T.al[:, CAP * rank:CAP * rank + CAP], ffw, T.off[:, C - B:C]))
+    interleave(2, g)
+    e_aown = ev()
 
-    wait(V, e_qi)
-    e_pidx = one(V.tensor_scalar(T.pidx[:], T.p1[:, 0:64], float(N), -192.0, A.mult, A.add))
-    interleave(True, [V] if OPT["i1early"] else [V, SC])
-    interleave(False, [V, SC])
+    def own(q):
+        wait(q, e_off, e_ff)
+        inc(pick(q, T.al[:, CAP * rank:CAP * rank + CAP], ffw, T.off[:, C - B:C]), e_aown)
+    if OPT["ownv"] < 2:
+        own((SC, V)[OPT["ownv"]])
+
+    for q, early_parts in zip((SC, V), OPT["i1early"]):
+        for k in (1, 0, 2):
+            if k not in early_parts or q is V:
+                interleave(k, q)
+    if OPT["ownv"] == 2:
+        own(V)
     wait(V, e_i1, e_i0, cv)
     e_p = one(V.tensor_tensor_scan(T.pp[:], T.i0[:], T.i1[:], 0.0, A.mult, A.add))
+    if OPT["ownv"] == 3:
+        own(V)
     e_c = ev()
     for q, a, b in ((V, 0, OPT["cv"]), (SC, OPT["cv"], Q)):
         if a < b:
@@ -536,23 +632,35 @@ def rank_program(g, core, T, topo):
             inc(pick(q, T.d1[:, 2 * a:2 * b:2], T.pp[:, 0:8 * I], T.pidx[:, a // 16:b // 16]), e_c)
 
     aarr = [T.sem.aarr, landing(T, topo, rank, *aplan), 0]
+    edge = OPT["tail"]
+    parts = list(zip(edge, edge[1:]))
     e_a = []
-    for h, q in enumerate((V, SC)):
+    for h, (a, b) in enumerate(parts):
+        q = V if h == 0 and OPT["av"] else SC
         wait(q, aarr, e_aown)
-        e_a.append(one(pick(q, T.d1[:, Q * h + 1:Q * h + Q:2], T.al[:, 0:S], T.slot[:, 32 * h:32 * h + 32])))
+        e_a.append(one(pick(q, T.d1[:, 2 * a + 1:2 * b:2], T.al[:, 0:S], T.slot[:, a // 16:b // 16])))
     e_y = ev()
     wait(V, e_d0)
-    for h in range(2):
-        w, odd, half = slice(Q * h, Q * h + Q), slice(Q * h + 1, Q * h + Q, 2), slice(512 * h, 512 * h + 512)
+
+    def zeros(h):
+        a, b = parts[h]
         wait(V, e_a[h])
-        v(V.tensor_scalar(T.d0[:, odd], T.d1[:, odd], 0.0, None, A.is_equal))
-        wait(V, cv, e_c)
-        e_o = one(V.tensor_tensor_scan(T.oo[:, w], T.d0[:, w], T.d1[:, w], 0.0, A.mult, A.add))
-        q, d = ((SC, SC), (V, SY))[h]
+        return one(V.tensor_scalar(T.d0[:, 2 * a + 1:2 * b:2], T.d1[:, 2 * a + 1:2 * b:2], 0.0, None, A.is_equal))
+    e_m = [zeros(h) for h in range(OPT["ahead"])]
+    for h, (a, b) in enumerate(parts):
+        wait(V, e_m[h], e_c)
+        e_o = one(V.tensor_tensor_scan(T.oo[:, 2 * a:2 * b], T.d0[:, 2 * a:2 * b], T.d1[:, 2 * a:2 * b], 0.0, A.mult, A.add))
+        q = {"G": g, "S": SC, "V": V}[OPT["ysc"][h]]
+        if len(e_m) < len(parts):
+            e_m.append(zeros(len(e_m)))
         wait(q, e_o)
-        e_yo = one(copy(q, T.yo[:, half], T.oo[:, odd]))
+        if q is g:
+            e_yo = one(g.affine_select(T.yo[:, a:b], T.oo[:, 2 * a + 1:2 * b:2], [[0, b - a]], A.is_ge, 0.0, 0, 0))
+        else:
+            e_yo = one(copy(q, T.yo[:, a:b], T.oo[:, 2 * a + 1:2 * b:2]))
+        d = SC if h + 2 == len(parts) else SY
         wait(d, e_yo)
-        inc(d.dma_start(T.y[:, half], T.yo[:, half]), e_y, 16)
+        inc(d.dma_start(T.y[:, a:b], T.yo[:, a:b]), e_y, 16)
     wait(SY, e_y)
     for e in evs + [sent]:
         if e[1] > e[2]:

from concourse.bass import DstId, RemoteDMATransfer
from concourse.mybir import AluOpType as A, ActivationFunctionType as AF

N, M, I, Q, CAP = 8, 4096, 256, 1024, 192
S = N * CAP
C = S // 16
B = CAP // 16
BIG = 65536.0
BF, F16, F32, I32, U16 = "bfloat16", "float16", "float32", "int32", "uint16"

SCRATCH = {}
for _n, _w, _d in [
    ("zero", 512, BF), ("b128", 128, BF), ("l2", 128, BF), ("zz", 144, BF), ("zi", 144, BF), ("zt", 144, BF),
    ("id8", 128, BF), ("uu", 2048, F16), ("r0", 512, BF), ("m0", 512, BF), ("pent", 352, BF),
    ("cq", C, BF),
    ("tb", 272, I32), ("pm32", 256, I32), ("pm16", 256, U16),
    ("qtin", 64, I32), ("qn", 128, I32), ("qp", 192, BF), ("tc", 544, BF),
    ("src", Q, BF), ("qwin", S, BF), ("stwin", 272, BF), ("twin", M, BF), ("tg", M, BF),
    ("s1", 128, BF), ("sw", 128, BF), ("ee", 512, BF), ("cin", 512, BF), ("mx", 512, F32),
    ("slot", 64, U16), ("qs", 2 * C, F16), ("qr", 2 * C, F16),
    ("se", 48, I32), ("w1", 80, I32), ("w2", 112, I32), ("li", 112, U16),
    ("xw", M, BF), ("xs", M, BF), ("mk", M + 368, BF), ("ff", M + 16, BF),
    ("pen", 768, BF), ("kk", 272, F32), ("tt", 768, F32),
    ("il", C, U16), ("trep", S, F32), ("pre", 768, F32), ("sc", 2 * S, BF), ("cc", S, BF),
    ("o1", C, F32), ("o2", C, F32), ("o3", C, F32), ("off", C, U16),
    ("ans", S, BF), ("al", S, BF), ("sl", 7 * I, BF), ("i0", 8 * I, BF), ("i1", 8 * I, BF), ("pp", 8 * I, BF),
    ("pidx", 64, U16), ("d0", 2 * Q, BF), ("d1", 2 * Q, BF), ("oo", 2 * Q, BF), ("yo", Q, BF),
]:
    SCRATCH[_n] = ("sbuf", [128, _w], _d)
for _k in range(8):
    SCRATCH["p%d" % _k] = ("psum", [128, 512], F32)

SEMAPHORES = ["qarr0", "qarr1", "sarr", "sarr1", "sarr2", "aarr", "sent"] + ["e%d" % _k for _k in range(140)]

OPT = {"xa": 1536, "ue": 2, "xsv": 1024, "relay": 0, "tfill": 2560, "groups": [4, 4], "qcalls": [4, 2],
       "tail": [0, 256, 640, 1024], "rep0": 0, "tat": 0, "xb": 1536, "xbat": 1, "tg0": 2048, "fill": 384,
       "slv": 1, "ownv": 3, "cv": 512, "ansv": 384, "ic": ["SSS", "SS", "VSS"], "x0": 512, "f0": 2, "c0": 256, "ahead": 2, "piece": 128, "wide": 1,
       "s1first": 0, "pmat": 1, "direct": 0, "i0": "S", "pre": 0, "ilfirst": 0, "align": 0, "ansv0": 0, "d0": 0, "xq": 512, "tgv": 0, "av": 1, "ysc": "GSV", "penv": 1, "i1early": [[1, 0], [1, 0]], "uw": 1536, "xfirst": 1024}


def peers(T, topo, r):
    c = T.cores
    rot = [(r + k) % N for k in range(1, N)]
    far = [o for o in rot if topo.chip(c[o]) != topo.chip(c[r])]
    near = [o for o in rot if topo.chip(c[o]) == topo.chip(c[r])]
    return far, near


def bits(engines):
    return sum(1 << e for e in engines)


def engines_of(T, topo, r):
    c = T.cores
    far, near = peers(T, topo, r)
    off = topo.engines(c[r], c[far[0]])
    return off, [e for e in topo.engines(c[r], c[near[0]]) if e not in off]


def share(dests, engines):
    n = len(dests)
    return [(o, engines[k * len(engines) // n:(k + 1) * len(engines) // n]) for k, o in enumerate(dests)]


def calls_of(T, topo, r, sizes, near_call, near_engines, back=False):
    far, near = peers(T, topo, r)
    if back:
        far = blocks(T, topo, r)[:len(far)]
    off, on = engines_of(T, topo, r)
    first = [sum(sizes[:k]) for k in range(len(sizes) + 1)]
    return [share(far[a:b], off) + (share(near, on[:near_engines]) if k == near_call else [])
            for k, (a, b) in enumerate(zip(first, first[1:]))]


def landing(T, topo, rank, *plan):
    return sum(len(e) for r in range(N) for call in calls_of(T, topo, r, *plan) for o, e in call if o == rank)


def blocks(T, topo, o):
    far, near = peers(T, topo, o)
    return sorted(far, key=lambda r: peers(T, topo, r)[0].index(o)) + near + [o]


def rank_program(g, core, T, topo):
    rank = T.rank_of(core)
    if rank is None:
        return
    V, SC, PE, SY = g.vector, g.scalar, g.tensor, g.sync
    evs = []

    def ev():
        e = [T.sem["e%d" % len(evs)], 0, 0]
        evs.append(e)
        return e

    def inc(ins, e, n=1):
        ins.then_inc(e[0], n)
        e[1] += n
        return e

    def one(ins, n=1):
        return inc(ins, ev(), n)

    seen = [(q, []) for q in (g, V, SC, PE, SY)]

    def wait(q, *es):
        mine = [s for k, s in seen if k is q][0]
        for e in es:
            if e[1] > 0 and not [1 for f, n in mine if f is e and n == e[1]]:
                q.wait_ge(e[0], e[1])
                mine.append((e, e[1]))
                e[2] = e[1]

    cv, cg = ev(), ev()

    def v(ins):
        inc(ins, cv)

    def vs():
        wait(V, cv)

    def dst(o):
        a = topo.addr(T.cores[o])
        return DstId(rid=a[0], pnc=a[1])

    sent = [T.sem.sent, 0, 0]

    def fused(items):
        g.remote_dma_fused([RemoteDMATransfer(dst_ids=[dst(o) for o in os_], dma_engine_mask=bits(en), remote_sem=sem,
                                              srcs=[s], dsts=ds) for os_, en, s, ds, sem in items],
                           local_sem=sent[0])
        sent[1] += sum(len(item[1]) for item in items)

    def wrap(out, rhs_of, e, first=True, last=True, z=T.zz):
        for r in range(16):
            inc(PE.matmul(out, z[:, 15 - r:143 - r], rhs_of(r), first and r == 0, last and r == 15), e)
        return e

    def pick(q, out, win, lst):
        return V.tensor_copy(out, win.indirect(lst)) if q is V else SC.activation(out, win.indirect(lst), AF.Copy)

    def copy(q, out, in_):
        return V.tensor_copy(out, in_) if q is V else SC.activation(out, in_, AF.Copy)

    def cuts(a, b, n):
        return [(k, min(k + n, b)) for k in range(a, b, n)]

    far, near = peers(T, topo, rank)
    off, on = engines_of(T, topo, rank)

    e_qtin, e_qn, e_tb, e_pm, e_x = ev(), ev(), ev(), ev(), ev()
    inc(SY.dma_start(T.qn[:, 0:64], T.qt[:]), e_qn, 16)
    inc(SC.dma_start(T.qn[:, 64:128], T.qi[:]), e_qn, 16)
    inc(SY.dma_start(T.tb[:, 0:256], T.times[:]), e_tb, 16)
    inc(SC.dma_start(T.tb[:, 256:272], T.starts[:, 0:I]), e_tb, 16)
    for blk in range(2):
        for g2 in range(2):
            k = blk * 32 + g2 * 16
            inc((SY, SC)[g2].dma_start(T.qtin[:, k:k + 16], T.qt[g2::2, 512 * blk:512 * blk + 512]), e_qtin, 16)
    inc(SC.dma_start(T.pm32[:], T.pm[:]), e_pm, 16)
    XA = OPT["xa"]
    inc(SY.dma_start(T.xw[:, 0:XA], T.x[:, 0:XA]), e_x, 16)

    e_zero = one(V.memset(T.zero[:], 0.0))
    e_z0 = ev()
    for z in (T.zz, T.zi, T.zt):
        inc(V.memset(z[:], 0.0), e_z0)
    v(V.memset(T.m0[:], 1.0))
    e_w0 = one(V.memset(T.stwin[:, 0:I], 0.0))
    e_st256 = one(V.memset(T.stwin[:, I:272], float(M // 16)))
    vs()
    v(V.memset(T.m0[:, 0::8], 0.0))
    e_tw0 = one(V.memset(T.twin[:, 0:OPT["tfill"]], 0.0))

    def clear(ap, n):
        return g.affine_select(ap, T.zero[:, 0:n], [[0, n]], A.is_ge, 0.0, 0, 0)
    wait(g, e_zero)
    blk16 = [[-16, 8], [0, 16]]
    inc(g.affine_select(T.b128[:], T.zero[:, 0:128], blk16, A.is_ge, 1.0, -16, 1), cg)
    inc(g.affine_select(T.l2[:], T.zero[:, 0:128], [[1, 128]], A.is_ge, -1.0, 0, -1), cg)
    e_r0 = one(g.iota(T.r0[:], [[-B, N], [256, 64]], (N - 1) * B, 0, allow_small_or_imprecise_dtypes=True))
    wait(g, cg)
    e_b128 = one(g.affine_select(T.b128[:], T.b128[:], blk16, A.is_ge, 0.0, 0, 1))
    inc(g.affine_select(T.l2[:], T.l2[:], [[16, 8], [0, 16]], A.is_ge, 0.0, 15, -1), cg)
    wait(g, cg)
    e_l2 = one(g.affine_select(T.l2[:], T.l2[:], [[-1, 128]], A.not_equal, 2048.0, 0, 1))
    wait(g, e_z0, e_b128)
    e_z = ev()
    inc(g.affine_select(T.zz[:, 15:143:16], T.b128[:, 0::16], [[0, 8]], A.is_ge, 0.0, 0, 0), e_z)
    inc(g.affine_select(T.zi[:, 15:143:16], T.zero[:, 0:8], [[-16, 8]], A.not_equal, 1.0, 0, 1), e_z)
    inc(g.affine_select(T.zt[:, 15:143:16], T.b128[:, 0::16], [[-16, 8]], A.not_equal, 0.0, 0, 1), e_z)
    e_cq = one(g.iota(T.cq[:], [[-M // 16, N], [0, B]], -M // 32, 0, allow_small_or_imprecise_dtypes=True))
    e_pad = ev()
    inc(g.iota(T.se[:, 32:48], [[16, 16]], M, 1), e_pad)
    inc(clear(T.ff[:, 0:1], 1), e_pad)
    inc(clear(T.kk[:, 256:272], 16), e_pad)
    inc(g.affine_select(T.pent[0:16, 0:272], T.zero[0:16, 0:272], [[0, 17], [-1, 16]], A.is_ge, BIG, 0, 1), cg)
    e_p16 = ev()
    inc(g.affine_select(T.pent[0:16, 272:352], T.zero[0:16, 0:80], [[1, 80]], A.is_ge, BIG, -33, -1), e_p16)
    wait(g, cg)
    inc(g.affine_select(T.pent[0:16, 0:272], T.pent[0:16, 0:272], [[1, 17], [0, 16]], A.is_ge, BIG, -1, -1), e_p16)
    e_u = ev()

    def make_u(k):
        inc(g.affine_select(T.uu[:, 512 * k:512 * k + 512], T.zero[:], [[-1, 4], [-16, 8], [0, 16]],
                            A.not_equal, 1.0, -4 * k, 1), e_u)
    for k in range(OPT["ue"]):
        make_u(k)

    wait(SC, e_zero)
    e_qw0, e_s0 = ev(), ev()
    for a, b in cuts(0, Q, 512):
        inc(copy(SC, T.src[:, a:b], T.zero[:]), e_s0)
    XB = OPT["xb"]
    if OPT["xbat"] == 0 and XA < XB:
        inc(SC.dma_start(T.xw[:, XA:XB], T.x[:, XA:XB]), e_x, 16)
    for a, b in cuts(OPT["tfill"], M, 512):
        inc(copy(SC, T.twin[:, a:b], T.zero[:, 0:b - a]), e_tw0)
    if OPT["xbat"] == 1 and XA < XB:
        inc(SC.dma_start(T.xw[:, XA:XB], T.x[:, XA:XB]), e_x, 16)
    for a, b in cuts(0, S, 512):
        inc(copy(SC, T.qwin[:, a:b], T.zero[:]), e_qw0)
    e_i0 = ev()

    e_tw = ev()

    e_stw, e_src, e_s1 = ev(), ev(), ev()
    wait(V, e_qn)
    e_hi = one(V.tensor_copy(T.qp[:, 0:128], T.qn[:]))
    wait(V, e_tb)
    e_t1 = one(V.tensor_copy(T.tc[:, 0:272], T.tb[:]))
    wait(V, e_hi)
    e_lo = one(V.tensor_tensor(T.qp[:, 128:192], T.qn[:, 0:64], T.qp[:, 0:64], A.subtract))

    def slices():
        wait(V, e_qtin)
        for k in range(2):
            inc(V.tensor_scalar(T.s1[:, 64 * k:64 * k + 64], T.qtin[:], 1.0 / 4096, 191.5 + k + 1.0 / 8192, A.mult, A.add), e_s1)
    slices()
    wait(V, e_t1)
    e_t2 = one(V.tensor_tensor(T.tc[:, 272:408], T.tb[:, 0:136], T.tc[:, 0:136], A.subtract))
    wait(V, e_s1)
    e_sw = one(V.transpose(T.sw[:], T.s1[:]))
    inc(V.tensor_tensor(T.tc[:, 408:544], T.tb[:, 136:272], T.tc[:, 136:272], A.subtract), e_t2)
    wait(SY, e_s0, e_hi)
    for k, a in enumerate((64, 0, 128)):
        if k == 2:
            wait(SY, e_lo)
        inc(SY.dma_start(T.src[k::16, :], T.qp[:, a:a + 64]), e_src, 16)
    wait(SY, e_tw0, e_w0, e_t1, e_t2)
    for k in range(2):
        inc(SY.dma_start(T.twin[k::16, :], T.tc[:, 272 * k:272 * k + 256]), e_tw, 16)
    for k in range(2):
        inc(SY.dma_start(T.stwin[k::16, 0:I], T.tc[:, 272 * k + 256:272 * k + 272]), e_stw, 16)
    if XB < M:
        inc(SY.dma_start(T.xw[:, XB:M], T.x[:, XB:M]), e_x, 16)

    wait(V, e_sw)
    e_e = ev()
    for k in range(0, N, 2):
        inc(V.tensor_scalar(T.ee[:, 64 * k:64 * k + 128], T.sw[:], float(192 + N - 1 - k), None, A.is_equal), e_e)
    wait(V, e_pm)
    e_pm16 = one(V.tensor_copy(T.pm16[:], T.pm32[:]))
    wait(V, e_e, e_r0)
    e_cin = one(V.tensor_tensor_scan(T.cin[:], T.r0[:], T.ee[:], 1024.0, A.min, A.add))
    wait(PE, e_b128, e_l2, e_e, e_cin)
    e_d = ev()
    for k in range(N):
        inc(PE.matmul(T.p0[:, k::8], T.l2[:], T.ee[:, 64 * k:64 * k + 64], True, False), e_d)
        inc(PE.matmul(T.p0[:, k::8], T.b128[:], T.cin[:, 64 * k:64 * k + 64], False, True), e_d)
    e_d0 = ev()
    spare = [(T.d0[:, a:a + 512:2], e_d0) for a in range(0, 2 * Q, 512)] + [(T.i0[:, 0::8], e_i0), (T.i1[:, 0::8], e_i0)]

    def fill(n=1):
        for ap, e in [spare.pop(0) for _ in range(min(n, len(spare)))]:
            inc(V.memset(ap, 0.0), e)
    fill(OPT["f0"])
    wait(V, e_d, cv)
    v(V.tensor_tensor_scan(T.mx[:], T.m0[:], T.p0[:], 0.0, A.mult, A.max))
    fill()
    vs()
    e_slot = one(V.tensor_scalar(T.slot[:], T.mx[:, 7::8], -2049.0, None, A.add))
    fill()
    wait(V, e_slot, e_src, e_qw0)
    e_scat = one(V.tensor_copy(T.qwin[:, 0:S].indirect(T.slot[:, 0:64]), T.src[:]))

    wait(PE, e_z, e_stw, e_st256)
    e_se = ev()
    wrap(T.p6[:, 0:16], lambda r: T.stwin[:, r:I:16], e_se)
    wrap(T.p6[:, 16:32], lambda r: T.stwin[:, r + 1:I + 1:16], e_se)
    wait(PE, e_scat, e_cq)
    e_qwrap = wrap(T.p1[:, 0:2 * C:2], lambda r: T.qwin[:, r::16], ev(), z=T.zi)
    inc(PE.matmul(T.p1[:, 1:2 * C:2], T.b128[:], T.cq[:], True, False), e_qwrap)
    wrap(T.p1[:, 1:2 * C:2], lambda r: T.qwin[:, r::16], e_qwrap, first=False, z=T.zt)
    wait(SY, e_p16)
    e_pent = ev()
    for k in range(1, 8):
        inc(SY.dma_start(T.pent[16 * k:16 * k + 16, :], T.pent[0:16, :]), e_pent, 16)

    xw, tw = T.xw[:, 0:M], T.twin[:, 0:M]
    e_xs, e_tg = [], []

    def times_of(a, b, q=SC):
        wait(q, e_tw, e_pm16)
        e_tg.append((a, b, one(pick(q, T.tg[:, a:b], tw, T.pm16[:, a // 16:b // 16]))))
    for a, b in cuts(0, OPT["tg0"], 1024):
        times_of(a, b)

    def ticks_of(q, a, b):
        wait(q, e_x, e_pm16)
        e_xs.append((a, b, one(pick(q, T.xs[:, a:b], xw, T.pm16[:, a // 16:b // 16]))))
    for a, b in cuts(0, M - OPT["xsv"], 1024):
        ticks_of(SC, a, b)
    nsc = len(e_xs)

    def mask(k):
        a, b, e = e_xs[k]
        wait(V, e)
        inc(V.tensor_scalar(T.mk[:, a:b], T.xs[:, a:b], 0.0, None, A.is_equal), e_mk)
    e_mk = ev()

    wait(V, e_se)
    v(V.tensor_copy(T.se[:, 0:32], T.p6[:, 0:32]))
    XV = M - OPT["xsv"]
    ticks_of(V, XV, XV + OPT["x0"])
    wait(V, cv, e_pad)
    st, en = T.se[:, 0:16], T.se[:, 16:32]
    e_lists = ev()

    def part(t, k, n=1):
        return t[:, 16 * k:16 * (k + n)]

    def lists(level):
        vs()
        if level == 0:
            v(V.tensor_scalar(part(T.w1, 0), st, 0x1FF0, None, A.bitwise_and))
            v(V.tensor_tensor(part(T.w1, 2), en, st, A.not_equal))
            v(V.tensor_tensor(part(T.w1, 3), en, st, A.is_equal))
            v(V.tensor_scalar(part(T.w2, 4), st, 4, None, A.arith_shift_right))
            v(V.tensor_scalar(part(T.w1, 1), st, 15, None, A.bitwise_and))
        if level == 1:
            v(V.tensor_tensor(part(T.w2, 3), en, part(T.w1, 0), A.subtract))
            v(V.tensor_tensor(part(T.w2, 0, 2), part(T.w1, 2, 2), T.se[:, 16:48], A.mult))
            for k in (1, 2):
                v(V.tensor_scalar(part(T.w2, 4 + k), part(T.w2, 4), float(k), None, A.add))
        if level == 2:
            v(V.tensor_scalar(part(T.w1, 4), part(T.w2, 3), 16.0, 16.0, A.min, A.mult))
            v(V.tensor_tensor(part(T.w2, 1), part(T.w2, 1), st, A.max))
        if level == 3:
            v(V.tensor_tensor(part(T.w2, 2), part(T.w1, 4), part(T.w1, 1), A.add))
        if level == 4:
            inc(V.tensor_copy(T.li[:], T.w2[:]), e_lists)
    lists(0)
    ticks_of(V, XV + OPT["x0"], M)

    wait(V, e_qwrap)
    e_qs = one(V.tensor_copy(T.qs[:], T.p1[:, 0:2 * C]))
    wait(SY, e_qs)
    e_qown = one(SY.dma_start(T.qr[:, 14 * B:16 * B], T.qs[:, 2 * B * rank:2 * B * rank + 2 * B]), 16)
    wait(g, e_qs)
    qplan = (OPT["qcalls"], len(OPT["qcalls"]) - 1, 2)
    for k, call in enumerate(calls_of(T, topo, rank, *qplan)):
        at = [2 * B * blocks(T, topo, o).index(rank) for o, _ in call]
        fused([([o], e, T.qs[:, 2 * B * o:2 * B * o + 2 * B], [T.qr[:, p:p + 2 * B]], T.sem["qarr%d" % min(k, 1)])
               for (o, e), p in zip(call, at)])
    q0 = len(off) if len(OPT["qcalls"]) > 1 else landing(T, topo, rank, *qplan)
    qarr = [[T.sem.qarr0, q0, 0], [T.sem.qarr1, landing(T, topo, rank, *qplan) - q0, 0]]
    for k in range(OPT["ue"], 4):
        make_u(k)
    e_id = one(g.affine_select(T.id8[:], T.zero[:, 0:128], [[-1, 128]], A.not_equal, 1.0 / N, 0, 1))

    rest = list(range(nsc, len(e_xs))) + list(range(nsc))
    for level in range(1, 5):
        lists(level)
        mask(rest.pop(0))
    for k in rest:
        mask(k)

    e_pen = ev()
    pens = [(k, a, lst) for k, (a, lst) in enumerate(((0, 2), (288, 3), (272, 3)))]

    def penalty(q):
        k, a, lst = pens.pop()
        wait(q, e_lists, e_pent, e_p16)
        inc(pick(q, T.pen[:, I * k:I * k + I], T.pent[:, a:352], part(T.li, lst)), e_pen)
    if OPT["penv"] > 0:
        penalty(V)
    else:
        fill()
    wait(V, e_mk, e_lists)
    v(V.tensor_copy(T.mk[:, 0:M + 368].indirect(part(T.li, 1)), T.zero[:, 0:I]))
    if OPT["penv"] > 1:
        penalty(V)
    else:
        fill()
    vs()
    e_ff = one(V.tensor_tensor_scan(T.ff[:, 1:M + 1], T.mk[:, 0:M], T.xs[:], 0.0, A.mult, A.add))
    fill()
    ffw = T.ff[:, 0:M + 1]
    e_sown = ev()
    die = [topo.die(c) for c in T.cores]

    def held(r):
        far_, near_ = peers(T, topo, r)
        parts = ([s for s in far_ if die[s] == die[r]], [r] + near_, [s for s in far_ if die[s] != die[r]])
        if OPT["direct"]:
            parts = ([], [r] + near_, far_)
        return [[s for s in p if s < N - 1] for p in parts]

    def column(r, s):
        return I * sum(held(r), []).index(s)

    def lasts(r, slices):
        return T.sl[:, column(r, slices[0]):column(r, slices[0]) + I * len(slices)]

    def last_values(q):
        if rank < N - 1:
            mine = lasts(rank, [rank])
            wait(q, e_ff, e_lists, e_pad)
            inc(pick(q, mine, ffw, part(T.li, 0)), e_sown)
            wait(g, e_sown)
            to = [o for o in far if die[o] == die[rank] or OPT["direct"]]
            fused([(to, off, mine, [lasts(o, [rank]) for o in to], T.sem.sarr2 if OPT["direct"] else T.sem.sarr),
                   (near, on, mine, [lasts(near[0], [rank])], T.sem.sarr1)])
    if OPT["slv"]:
        last_values(V)

    e_kw = ev()
    for a, b in cuts(OPT["tg0"], M - OPT["tgv"], 1024):
        times_of(a, b)
    if OPT["tgv"]:
        times_of(M - OPT["tgv"], M, V)
    for a, b, e in e_tg:
        wait(PE, e)
        wrap(T.p5[:, a // 16:b // 16], lambda r: T.tg[:, a + r:b:16], e_kw)
    while pens:
        penalty(SC)
    wait(SC, e_kw)
    e_kk = one(SC.activation(T.kk[:, 0:256], T.p5[:, 0:256], AF.Identity, bias=-float(rank * M + M // 2)))
    if not OPT["slv"]:
        last_values(SC)
    early = CAP * OPT["qcalls"][0] if len(OPT["qcalls"]) > 1 else S - 16
    banks = [(p, a, b) for p, (a, b) in zip((T.p2, T.p3, T.p4, T.p6),
                                            cuts(0, early, 512) + cuts(early, S, 512) if OPT["align"] else cuts(0, S, 512))]
    e_tr = []

    def unwrap(upto):
        while len(e_tr) < len(banks) and banks[len(e_tr)][1] < upto:
            p, a, b = banks[len(e_tr)]
            wait(PE, e_u, e_lists, qarr[0], *([] if b <= early else [qarr[1], e_qown]))
            e_tr.append(ev())
            for r in range(16):
                inc(PE.matmul(p[:, r:b - a:16], T.uu[:, 128 * r:128 * r + 128], T.qr[:, a // 8 + 1:b // 8:2], True, True), e_tr[-1])
    unwrap(OPT["uw"])

    sizes = OPT["groups"]
    K = len(sizes)
    first = [CAP * sum(sizes[:k]) for k in range(K + 1)]
    chunks = list(zip(first, first[1:]))

    def pick_starts(q, k):
        a, b = chunks[k]
        wait(q, e_il[-1], e_stw, e_st256)
        return one(pick(q, T.sc[:, 2 * a:a + b], T.stwin[:, 0:272], T.il[:, a // 16:b // 16]))

    def instruments(k):
        a, b = ((0, early), (early, S))[k]
        wait(V, qarr[k], e_qown)
        e_il.append(one(V.tensor_copy(T.il[:, a // 16:b // 16], T.qr[:, a // 8:b // 8:2])))
    e_il = []
    if OPT["ilfirst"]:
        instruments(0)
    wait(V, e_lists, e_pen, e_kk)
    v(V.tensor_tensor(T.tt[:], T.kk[:, 0:272].indirect(part(T.li, 4, 3)), T.pen[:], A.add))
    if not OPT["ilfirst"]:
        instruments(0)
    fill(9)
    vs()
    v(V.tensor_tensor(T.tt[:, 0:256], T.tt[:, 0:256], T.tt[:, 512:768], A.min))

    aplan = (sizes[:-1] + [sizes[-1] - 2], K - 1, len(on), True)
    acalls = calls_of(T, topo, rank, *aplan)
    cbank = (T.p0, T.p7, T.p5)
    spread = []

    def times(k):
        unwrap(chunks[k][1])
        while len(spread) < len(banks) and banks[len(spread)][1] < chunks[k][1]:
            p, a, b = banks[len(spread)]
            wait(SC, e_tr[len(spread)])
            spread.append(one(copy(SC, T.trep[:, a:b], p[:, 0:b - a])))
        return list(spread)

    def compare(out, w, a, b, e):
        return inc(V.tensor_tensor(out, T.tt[:, w:w + 256].indirect(T.il[:, a // 16:b // 16]), T.trep[:, a:b], A.is_le), e)

    def offsets(k, e, between):
        a, b = chunks[k]
        n = (b - a) // 16
        c = slice(a // 16, b // 16)
        steps = (lambda: V.tensor_scalar(T.o1[:, c], cbank[k][:, n:2 * n], 8192.0, None, A.mult),
                 lambda: V.tensor_tensor(T.o2[:, c], T.o1[:, c], cbank[k][:, 0:n], A.min),
                 lambda: V.tensor_tensor(T.o3[:, c], T.o2[:, c], cbank[k][:, n:2 * n], A.add),
                 lambda: V.tensor_copy(T.off[:, c], T.o3[:, c]))
        for step in steps:
            if between:
                between.pop(0)()
            wait(V, e)
            e = one(step())
        return e

    sarr = [T.sem.sarr, len(off) * len(held(rank)[0]), 0]
    sarr1 = [T.sem.sarr1, len(on) * (near[0] < N - 1), 0]
    wide = off + on if OPT["wide"] else on
    sarr2 = [T.sem.sarr2, len(off) * len(held(rank)[2]) if OPT["direct"] else len(wide), 0]

    def relay():
        if OPT["direct"]:
            return
        wait(g, sarr)
        fused([(near, wide, lasts(rank, held(rank)[0]), [lasts(near[0], held(rank)[0])], T.sem.sarr2)])
        interleave(0, g)

    e_i1 = ev()

    def interleave(part, q):
        for s, who in zip(held(rank)[part], OPT["ic"][part]):
            came = ((sarr,), (sarr1, e_sown), (sarr2,))[part]
            if q is {"G": g, "S": SC, "V": V}[who]:
                wait(q, *came)
                if q is g:
                    inc(g.affine_select(T.i1[:, s + 1::8], lasts(rank, [s]), [[0, I]], A.is_ge, 0.0, 0, 0), e_i1)
                else:
                    inc(copy(q, T.i1[:, s + 1::8], lasts(rank, [s])), e_i1)
            if q is V and s not in marked:
                mark(part, s)

    marked = []

    def mark(part, s):
        marked.append(s)
        wait(V, *((sarr,), (sarr1, e_sown), (sarr2,))[part])
        inc(V.tensor_scalar(T.i0[:, s + 1::8], lasts(rank, [s]), 0.0, None, A.is_equal), e_i1)

    def answers(k, e):
        a, b = chunks[k]
        b = min(b, S - CAP)
        cut = b - (OPT["ansv"] if k == K - 1 else OPT["ansv0"])
        e_a = ev()
        for q, a_, b_ in ((SC, a, cut), (V, cut, b)):
            if a_ < b_:
                wait(q, e, e_ff, e_pad)
                inc(pick(q, T.ans[:, a_:b_], ffw, T.off[:, a_ // 16:b_ // 16]), e_a)
        if k == OPT["relay"]:
            relay()
        wait(g, e_a)
        mine = blocks(T, topo, rank)
        fused([([o], en_, T.ans[:, CAP * mine.index(o):CAP * mine.index(o) + CAP],
                [T.al[:, CAP * rank:CAP * rank + CAP]], T.sem.aarr) for o, en_ in acalls[k]])

    interleave(1, g)
    wait(PE, e_id, e_qs)
    e_qi = wrap(T.p1[:, 0:64], lambda r: T.src[:, r::16], ev(), last=False, z=T.zi)
    inc(PE.matmul(T.p1[:, 0:64], T.id8[:], T.sw[:, 0:64], False, True), e_qi)
    wait(PE, e_kk)
    e_n = None
    e_rep = times(0)
    times(OPT["rep0"])
    e_sg = pick_starts(SC, 0)
    for k in range(K):
        wait(V, e_il[-1], *e_rep)
        a, b = chunks[k]
        eb, a2 = ev(), a + (0 if k else OPT["c0"])
        if a < a2:
            compare(T.cc[:, a:a2], 256, a, a2, eb)
        vs()
        n, mid = (b - a) // 16, min(b, a + OPT["fill"]) if k else b
        ea = compare(T.sc[:, a + b:b + mid], 0, a, mid, ev())
        if k == 0:
            instruments(1)
        rest_ = [lambda lo=lo, hi=hi: compare(T.sc[:, b + lo:b + hi], 0, lo, hi, ea) for lo, hi in cuts(mid, b, OPT["piece"])]
        e_off = offsets(k - 1, e_n, [lambda: None] + rest_ if OPT["piece"] < 384 else []) if k else None
        if OPT["piece"] >= 384 and mid < b:
            compare(T.sc[:, b + mid:2 * b], 0, mid, b, ea)
        if k + 1 < K:
            e_rep = times(k + 1)
        if k:
            answers(k - 1, e_off)
        wait(PE, e_sg, ea)
        e_st = wrap(cbank[k][:, 0:2 * n], lambda r: T.sc[:, 2 * a + r:2 * b:16], ev(), True, False)
        if k + 1 < K:
            e_sg = pick_starts(SC, k + 1)
        wait(PE, compare(T.cc[:, a2:b], 256, a2, b, eb))
        e_n = wrap(cbank[k][:, 0:n], lambda r: T.cc[:, a + r:b:16], e_st, False, True)
    for k in OPT["i1early"][0]:
        interleave(k, SC)
    marks = [lambda k=k, s=s: mark(k, s) for k in OPT["i1early"][1] for s in held(rank)[k]]
    wait(V, e_qi)
    marks.append(lambda: inc(V.tensor_scalar(T.pidx[:], T.p1[:, 0:64], float(N), -192.0, A.mult, A.add), e_pidx))
    e_pidx = ev()
    while len(marks) > 5:
        marks.pop(0)()
    e_off = offsets(K - 1, e_n, marks)
    while marks:
        marks.pop(0)()
    answers(K - 1, e_off)
    if OPT["relay"] >= K:
        relay()
    interleave(2, g)
    e_aown = ev()

    def own(q):
        wait(q, e_off, e_ff)
        inc(pick(q, T.al[:, CAP * rank:CAP * rank + CAP], ffw, T.off[:, C - B:C]), e_aown)
    if OPT["ownv"] < 2:
        own((SC, V)[OPT["ownv"]])

    for q, early_parts in zip((SC, V), OPT["i1early"]):
        for k in (1, 0, 2):
            if k not in early_parts or q is V:
                interleave(k, q)
    if OPT["ownv"] == 2:
        own(V)
    wait(V, e_i1, e_i0, cv)
    e_p = one(V.tensor_tensor_scan(T.pp[:], T.i0[:], T.i1[:], 0.0, A.mult, A.add))
    if OPT["ownv"] == 3:
        own(V)
    e_c = ev()
    for q, a, b in ((V, 0, OPT["cv"]), (SC, OPT["cv"], Q)):
        if a < b:
            wait(q, e_p, e_pidx)
            inc(pick(q, T.d1[:, 2 * a:2 * b:2], T.pp[:, 0:8 * I], T.pidx[:, a // 16:b // 16]), e_c)

    aarr = [T.sem.aarr, landing(T, topo, rank, *aplan), 0]
    edge = OPT["tail"]
    parts = list(zip(edge, edge[1:]))
    e_a = []
    for h, (a, b) in enumerate(parts):
        q = V if h == 0 and OPT["av"] else SC
        wait(q, aarr, e_aown)
        e_a.append(one(pick(q, T.d1[:, 2 * a + 1:2 * b:2], T.al[:, 0:S], T.slot[:, a // 16:b // 16])))
    e_y = ev()
    wait(V, e_d0)

    def zeros(h):
        a, b = parts[h]
        wait(V, e_a[h])
        return one(V.tensor_scalar(T.d0[:, 2 * a + 1:2 * b:2], T.d1[:, 2 * a + 1:2 * b:2], 0.0, None, A.is_equal))
    e_m = [zeros(h) for h in range(OPT["ahead"])]
    for h, (a, b) in enumerate(parts):
        wait(V, e_m[h], e_c)
        e_o = one(V.tensor_tensor_scan(T.oo[:, 2 * a:2 * b], T.d0[:, 2 * a:2 * b], T.d1[:, 2 * a:2 * b], 0.0, A.mult, A.add))
        q = {"G": g, "S": SC, "V": V}[OPT["ysc"][h]]
        if len(e_m) < len(parts):
            e_m.append(zeros(len(e_m)))
        wait(q, e_o)
        if q is g:
            e_yo = one(g.affine_select(T.yo[:, a:b], T.oo[:, 2 * a + 1:2 * b:2], [[0, b - a]], A.is_ge, 0.0, 0, 0))
        else:
            e_yo = one(copy(q, T.yo[:, a:b], T.oo[:, 2 * a + 1:2 * b:2]))
        d = SC if h + 2 == len(parts) else SY
        wait(d, e_yo)
        inc(d.dma_start(T.y[:, a:b], T.yo[:, a:b]), e_y, 16)
    wait(SY, e_y)
    for e in evs + [sent]:
        if e[1] > e[2]:
            wait(g, e)
